import numpy as np
import ml_dtypes


def mxq(x, axis, fmt="e4m3"):
    dtype, down = {"e4m3": (ml_dtypes.float8_e4m3fn, 7), "e5m2": (ml_dtypes.float8_e5m2, 14)}[fmt]
    v = np.moveaxis(np.asarray(x, np.float32).astype(ml_dtypes.bfloat16).astype(np.float64), axis, -1)
    blocks = v.reshape(v.shape[:-1] + (-1, 32))
    amax = np.abs(blocks).max(-1, keepdims=True)
    byte = np.maximum(np.where(amax > 0, np.frexp(amax)[1] - 1 + 127, 0) - down, 1)
    scale = np.exp2(byte - 127.0)
    codes = (blocks / scale).astype(np.float32).astype(dtype).astype(np.float64)
    return np.moveaxis((codes * scale).reshape(v.shape), -1, axis)


WIDE = False


def mx_kscale(k):
    if not WIDE:
        return np.ones(k)
    levels = np.array([10, -10, 5, -5, 0])
    if k % 512:
        return np.exp2(np.random.permutation(np.resize(levels, k // 32))).repeat(32)
    a = np.empty((k // 512, 16))
    for p in range(k // 512):
        a[p, :8] = np.random.permutation(np.resize(levels, 8))
        for g in range(8):
            far = levels[np.abs(levels - a[p, g]) >= 10]
            a[p, g + 8] = far[np.random.randint(len(far))]
    return np.exp2(a.ravel()).repeat(32)


def f64(x):
    return np.asarray(x).astype(np.float64)


def striped(idx):
    return np.tile(idx.reshape(-1, 16).T, (8, 1)).astype(np.uint16)


def unstriped(offs):
    return offs[:16].T.reshape(-1).astype(np.int64)


def striped8(idx):
    return np.concatenate([x.reshape(-1, 16).T for x in idx]).astype(np.uint16)


def runs(offs, k):
    lists = np.stack([offs[16 * r : 16 * r + 16].T.reshape(-1) for r in range(8)]).astype(np.int64)
    return lists[np.arange(k) % 512 // 64]


def pack_weight(w):
    k, n = w.shape
    w = f64(np.asarray(w, np.float32).astype(ml_dtypes.bfloat16)).reshape(k // 32, 32, n)
    amax = np.abs(w).max(1)
    byte = np.clip(np.where(amax > 0, np.frexp(amax)[1] - 1 + 127 - 7, 1), 1, 254)
    scaled = (w * np.exp2(127.0 - byte)[:, None, :]).reshape(k, n).astype(np.float32)
    words = np.ascontiguousarray(scaled.reshape(k // 512, 128, 4, n).transpose(0, 1, 3, 2)).astype(ml_dtypes.float8_e4m3fn).view(np.uint8)
    return words, np.ascontiguousarray(byte.astype(np.uint8).reshape(k // 512, 16, n))


def unpack_weight(words, scales):
    g, p, n, _ = words.shape
    vals = np.ascontiguousarray(words).view(ml_dtypes.float8_e4m3fn).astype(np.float64) * np.repeat(np.exp2(scales.astype(np.float64) - 127.0), 8, axis=1)[..., None]
    return vals.transpose(0, 1, 3, 2).reshape(g * 512, n)


def sigmoid(v):
    return 1.0 / (1.0 + np.exp(-np.maximum(v, -700.0)))

def planes(y):
    n, m = y.shape
    v = y.astype(np.float32).astype(ml_dtypes.bfloat16).astype(np.float64).reshape(n // 32, 32, m)
    top = np.abs(v).max(1)
    byte = np.clip(np.where(top > 0, np.frexp(top)[1] - 1 + 127 - 7, 1), 1, 254)
    codes = (v * np.exp2(127.0 - byte)[:, None, :]).reshape(n, m).astype(np.float32).astype(ml_dtypes.float8_e4m3fn).view(np.uint8)
    words = codes.reshape(n // 512, 128, 4, m).transpose(0, 1, 3, 2)
    return np.ascontiguousarray(words), np.ascontiguousarray(byte.astype(np.uint8).reshape(n // 512, 16, m))


K, T, S, V, N, H = 512, 2048, 512, 256, 512, 512


def setup_inputs():
    n = np.random.standard_normal
    s = mx_kscale(K)[:, None]
    u = mx_kscale(H)
    packed_xT = pack_weight(n((K, T)) * s)
    packed_w2 = pack_weight(n((K, H)) / np.sqrt(K) / s)
    packed_w3 = pack_weight(n((H, N)) / np.sqrt(H) / u[:, None])
    perm = np.stack([np.random.permutation(S) for _ in range(8)])
    return {
        "x_words": packed_xT[0],
        "x_scales": packed_xT[1],
        "w1": (n((K, H)) / np.sqrt(K) / s * u).astype(np.float32),
        "w2_words": packed_w2[0],
        "w2_scales": packed_w2[1],
        "w3_words": packed_w3[0],
        "w3_scales": packed_w3[1],
        "offs": striped(np.random.permutation(T)[:S]),
        "la": striped8(perm[:, :V]),
        "lb": striped8(perm[:, V:]),
    }


def reference(x_words, x_scales, w1, w2_words, w2_scales, w3_words, w3_scales, offs, la, lb):
    xq = unpack_weight(x_words, x_scales)[:, unstriped(offs)]
    y = mxq(f64(w1), 0, "e4m3").T @ xq
    b = y[np.arange(H)[:, None], runs(lb, H)]
    s = sigmoid(unpack_weight(w2_words, w2_scales).T @ xq)
    q = s[np.arange(H)[:, None], runs(la, H)]
    a = y[np.arange(H)[:, None], runs(la, H)]
    d = q * (b - a)
    nb = b - d
    na = a + d
    p = np.zeros((H, S))
    p[np.arange(H)[:, None], runs(la, H)] = na
    z = p.copy()
    z[np.arange(H)[:, None], runs(lb, H)] = nb
    out_0 = unpack_weight(w3_words, w3_scales).T @ mxq(z, 0, "e4m3")
    return (out_0,) + planes(out_0)

@@ -1,0 +1,212 @@
+from contextlib import ExitStack
+
+import concourse.mybir as mybir
+
+K, T, S, V, N, H = 512, 2048, 512, 256, 512, 512
+FLOPS = 2 * K * H * S * 2 + 2 * H * N * S
+
+F32 = mybir.dt.float32
+BF16 = mybir.dt.bfloat16
+I32 = mybir.dt.int32
+U32 = mybir.dt.uint32
+U16 = mybir.dt.uint16
+U8 = mybir.dt.uint8
+FP8X4 = mybir.dt.float8_e4m3fn_x4
+ALU = mybir.AluOpType
+ACT = mybir.ActivationFunctionType
+
+P = 128
+PACK = 4
+CH = 128
+
+
+def words_of(packed):
+    return packed[0].rearrange("p n t -> p (n t)").bitcast(I32)
+
+
+def tile_picked_swapgate_sigmoid_po_kernel(
+    tc, x_words, x_scales, w1, w2_words, w2_scales, w3_words, w3_scales, offs, la, lb, out_0, out_1, out_2
+):
+    nc = tc.nc
+    with ExitStack() as ctx:
+        keep = ctx.enter_context(tc.tile_pool(name="keep", bufs=1))
+        psum = ctx.enter_context(tc.psum_pool(name="psum", bufs=8))
+
+        def sb(name, shape, dtype):
+            return keep.tile(shape, dtype, name=name, align_bytes=64)
+
+        def bank(shape):
+            return psum.tile(shape, F32, name="bank")
+
+        offs_t = keep.tile([P, S // 16], U16, name="offs_t")
+        la_t = keep.tile([P, V // 16], U16, name="la_t")
+        lb_t = keep.tile([P, V // 16], U16, name="lb_t")
+        xw = sb("xw", [P, T], U32)
+        xs = sb("xs", [P, T], U8)
+        ws_raw = sb("ws_raw", [P, H], U8)
+        w2_raw = sb("w2_raw", [P, H], I32)
+        w3_raw = sb("w3_raw", [P, N], I32)
+        w1_raw = [sb("w1_raw%d" % h, [P, PACK, H // 2], F32) for h in range(2)]
+
+        warm = sb("warm", [P, 2], F32)
+        nc.vector.memset(xs[:].bitcast(I32), 0)
+        nc.gpsimd.memset(ws_raw[:].bitcast(I32), 0)
+        nc.gpsimd.memset(warm[:, 0:1], 0.0)
+        nc.scalar.activation(warm[:, 1:2], warm[:, 0:1], ACT.Sigmoid)
+
+        w1_rows = w1.rearrange("(p j) c -> p j c", j=PACK)
+        nc.sync.dma_start(w1_raw[0][:], w1_rows[:, :, 0 : H // 2])
+        for q in range(4):
+            nc.sync.dma_start(xs[32 * q : 32 * q + 4, :].bitcast(I32), x_scales[0, 4 * q : 4 * q + 4, :].bitcast(I32))
+        nc.sync.dma_start(offs_t[:], offs)
+        nc.sync.dma_start(w1_raw[1][:], w1_rows[:, :, H // 2 : H])
+        nc.sync.dma_start(xw[:].bitcast(I32), words_of(x_words))
+        nc.sync.dma_start(w2_raw[:], words_of(w2_words))
+        for row, scales, queue in ((0, w2_scales, nc.sync), (4, w3_scales, nc.gpsimd)):
+            for q in range(4):
+                queue.dma_start(
+                    ws_raw[32 * q + row : 32 * q + row + 4, :].bitcast(I32), scales[0, 4 * q : 4 * q + 4, :].bitcast(I32)
+                )
+        nc.sync.dma_start(la_t[:], la)
+        nc.sync.dma_start(lb_t[:], lb)
+        nc.sync.dma_start(w3_raw[:], words_of(w3_words))
+
+        gs = sb("gs", [P, S], U8)
+        nc.vector.tensor_copy(gs[:], xs[:].indirect(offs_t[:]))
+
+        w1_b = sb("w1_b", [P, H * PACK], BF16)
+        w1_v = w1_b[:].rearrange("p (t m j) -> p m t j", t=PACK, j=PACK)
+        for h in range(2):
+            nc.vector.tensor_copy(w1_v[:, 64 * h : 64 * h + 64], w1_raw[h][:].rearrange("p j (m t) -> p m t j", t=PACK))
+        w1_c = sb("w1_c", [P, H], U32)
+        w1_s = sb("w1_s", [P, H], U8)
+        nc.vector.quantize_mx(out=w1_c[:].bitcast(FP8X4), scales=w1_s[:], in_=w1_b[:])
+
+        gw = sb("gw", [P, S], U32)
+        for h in range(2):
+            nc.vector.tensor_copy(gw[:, 256 * h : 256 * h + 256], xw[:].indirect(offs_t[:, 16 * h : 16 * h + 16]))
+
+        def deal(dst, src):
+            nc.vector.tensor_copy(dst[:].rearrange("p (t m) -> p m t", t=PACK), src[:].rearrange("p (m t) -> p m t", t=PACK))
+
+        w2_c = sb("w2_c", [P, H], I32)
+        w3_c = sb("w3_c", [P, N], I32)
+        ws = keep.tile([P, H], U8, name="ws", tag="xw", align_bytes=64)
+        deal(w2_c, w2_raw)
+        deal(ws, ws_raw)
+
+        def mm(dst, lw, ls, t, rw, rs):
+            cols = slice(P * t, P * t + P)
+            nc.tensor.matmul_mx(
+                out=dst, lhsT=lw[:, cols].bitcast(FP8X4), lhsT_scale=ls[:, cols], rhs=rw.bitcast(FP8X4), rhs_scale=rs, start=True, stop=True
+            )
+
+        y = [sb("y%d" % t, [P, S], F32) for t in range(PACK)]
+        pre = [sb("pre%d" % t, [P, S], F32) for t in range(PACK)]
+        qq2 = [sb("qq%d" % u, [P, 2, 2, V], F32) for u in range(2)]
+        order = (2, 0, 1, 3)
+        qq = {t: qq2[i // 2][:, i % 2] for i, t in enumerate(order)}
+        a = [sb("a%d" % t, [P, V], F32) for t in range(PACK)]
+        e = [sb("e%d" % t, [P, V], F32) for t in range(PACK)]
+        df = [sb("df%d" % t, [P, 2, V], F32) for t in range(PACK)]
+        z = [sb("z%d" % t, [P, S], F32) for t in range(PACK)]
+        z_b = sb("z_b", [P, S, PACK], BF16)
+
+        def make_y(t, pieces):
+            width = S // pieces
+            for h in range(pieces):
+                cols = slice(width * h, width * h + width)
+                acc = bank([P, width])
+                mm(acc[:], w1_c[:], w1_s[:], t, gw[:, cols], gs[:, cols])
+                nc.scalar.copy(y[t][:, cols], acc[:])
+
+        def make_q(t):
+            acc = bank([P, S])
+            mm(acc[:], w2_c[:], ws[:], t, gw[:], gs[:])
+            nc.scalar.copy(pre[t][:], acc[:])
+            nc.scalar.activation(qq[t][:, 0, :], pre[t][:].indirect(la_t[:]), ACT.Sigmoid)
+
+        def one_minus(both):
+            nc.scalar.activation(both[:, :, 1, :], both[:, :, 0, :], ACT.Copy, bias=1.0, scale=-1.0)
+
+        def get_a(t):
+            nc.vector.tensor_copy(a[t][:], y[t][:].indirect(la_t[:]))
+
+        def get_e(t):
+            nc.vector.tensor_tensor(e[t][:], y[t][:].indirect(lb_t[:]), a[t][:], ALU.subtract)
+
+        def get_df(t):
+            nc.vector.tensor_tensor(df[t][:], qq[t], e[t][:].unsqueeze(1).to_broadcast([P, 2, V]), ALU.mult)
+
+        def put(t, which):
+            nc.vector.tensor_tensor(z[t][:].indirect((la_t, lb_t)[which][:]), a[t][:], df[t][:, which, :], ALU.add)
+
+        def weave(t):
+            for c in range(0, S, CH):
+                if c == 0 and t >= 2:
+                    nc.vector.tensor_copy(z_b[:, c : c + CH, t], z[t][:, c : c + CH])
+                else:
+                    nc.scalar.copy(z_b[:, c : c + CH, t], z[t][:, c : c + CH])
+
+        t0, t1, t2, t3 = order
+        make_y(t0, 2)
+        make_y(t1, 1)
+        make_q(t0)
+        one_minus(qq2[0][:, 0:1])
+        make_y(t2, 1)
+        make_q(t1)
+        one_minus(qq2[0][:, 1:2])
+        make_y(t3, 1)
+        make_q(t2)
+        make_q(t3)
+        one_minus(qq2[1][:])
+        get_a(t0)
+        deal(w3_c, w3_raw)
+        get_e(t0)
+        get_a(t1)
+        get_e(t1)
+        for i in range(2):
+            get_df(order[i])
+            get_a(order[i + 2])
+            put(order[i], 0)
+            get_e(order[i + 2])
+            put(order[i], 1)
+            weave(order[i])
+        get_df(t2)
+        get_df(t3)
+        put(t2, 0)
+        put(t3, 0)
+        put(t2, 1)
+        weave(t2)
+        put(t3, 1)
+        weave(t3)
+
+        z_c = sb("z_c", [P, S], U32)
+        z_s = sb("z_s", [P, S], U8)
+        o_b = sb("o_b", [P, S, PACK], BF16)
+        o_c = sb("o_c", [P, S], U32)
+        o_s = sb("o_s", [P, S], U8)
+        out_rows = out_0.rearrange("(p t) s -> p t s", t=PACK)
+        chunks = [slice(c, c + CH) for c in range(0, S, CH)]
+
+        def quant(codes, scales, src, cols):
+            nc.vector.quantize_mx(out=codes[:, cols].bitcast(FP8X4), scales=scales[:, cols], in_=src[:, cols, :].rearrange("p s t -> p (s t)"))
+
+        o = []
+        for i, cols in enumerate(chunks):
+            quant(z_c, z_s, z_b, cols)
+            acc = bank([P, PACK, CH])
+            for t in range(PACK):
+                mm(acc[:, t, :], w3_c[:], ws[4:P, :], t, z_c[:, cols], z_s[:, cols])
+            o.append(sb("o%d" % i, [P, PACK, CH], F32))
+            nc.scalar.copy(o[i][:], acc[:])
+            nc.sync.dma_start(out_rows[:, :, cols], o[i][:])
+        for i, cols in enumerate(chunks):
+            nc.vector.tensor_copy(o_b[:, cols, :], o[i][:].rearrange("p t s -> p s t"))
+            quant(o_c, o_s, o_b, cols)
+            if i % 2 == 1:
+                half = slice(CH * (i - 1), CH * (i + 1))
+                nc.sync.dma_start(words_of(out_1)[:, half], o_c[:, half].bitcast(I32))
+        for q in range(4):
+            queue = nc.scalar if q % 2 else nc.sync
+            queue.dma_start(out_2[0, 4 * q : 4 * q + 4, :].bitcast(I32), o_s[32 * q : 32 * q + 4, :].bitcast(I32))

@@ -18,6 +18,7 @@ ACT = mybir.ActivationFunctionType
 P = 128
 PACK = 4
 CH = 128
+WARM = 3
 
 
 def words_of(packed):
@@ -43,33 +44,35 @@ def tile_picked_swapgate_sigmoid_po_kernel(
         lb_t = keep.tile([P, V // 16], U16, name="lb_t")
         xw = sb("xw", [P, T], U32)
         xs = sb("xs", [P, T], U8)
-        ws_raw = sb("ws_raw", [P, H], U8)
+        w2s_raw = sb("w2s_raw", [P, H], U8)
+        w3s_raw = sb("w3s_raw", [P, N], U8)
         w2_raw = sb("w2_raw", [P, H], I32)
         w3_raw = sb("w3_raw", [P, N], I32)
         w1_raw = [sb("w1_raw%d" % h, [P, PACK, H // 2], F32) for h in range(2)]
 
         warm = sb("warm", [P, 2], F32)
         nc.vector.memset(xs[:].bitcast(I32), 0)
-        nc.gpsimd.memset(ws_raw[:].bitcast(I32), 0)
-        nc.gpsimd.memset(warm[:, 0:1], 0.0)
+        nc.vector.memset(warm[:, 0:1], 0.0)
+        nc.gpsimd.memset(w2s_raw[:].bitcast(I32), 0)
+        nc.vector.memset(w3s_raw[:].bitcast(I32), 0)
         nc.scalar.activation(warm[:, 1:2], warm[:, 0:1], ACT.Sigmoid)
+
+        def load_scales(queue, dst, scales):
+            for g in range(4):
+                queue.dma_start(dst[32 * g : 32 * g + 4, :].bitcast(I32), scales[0, 4 * g : 4 * g + 4, :].bitcast(I32))
 
         w1_rows = w1.rearrange("(p j) c -> p j c", j=PACK)
         nc.sync.dma_start(w1_raw[0][:], w1_rows[:, :, 0 : H // 2])
-        for q in range(4):
-            nc.sync.dma_start(xs[32 * q : 32 * q + 4, :].bitcast(I32), x_scales[0, 4 * q : 4 * q + 4, :].bitcast(I32))
+        load_scales(nc.sync, xs, x_scales)
         nc.sync.dma_start(offs_t[:], offs)
         nc.sync.dma_start(w1_raw[1][:], w1_rows[:, :, H // 2 : H])
         nc.sync.dma_start(xw[:].bitcast(I32), words_of(x_words))
-        nc.sync.dma_start(w2_raw[:], words_of(w2_words))
-        for row, scales, queue in ((0, w2_scales, nc.sync), (4, w3_scales, nc.gpsimd)):
-            for q in range(4):
-                queue.dma_start(
-                    ws_raw[32 * q + row : 32 * q + row + 4, :].bitcast(I32), scales[0, 4 * q : 4 * q + 4, :].bitcast(I32)
-                )
         nc.sync.dma_start(la_t[:], la)
         nc.sync.dma_start(lb_t[:], lb)
+        nc.sync.dma_start(w2_raw[:], words_of(w2_words))
+        load_scales(nc.gpsimd, w2s_raw, w2_scales)
         nc.sync.dma_start(w3_raw[:], words_of(w3_words))
+        load_scales(nc.sync, w3s_raw, w3_scales)
 
         gs = sb("gs", [P, S], U8)
         nc.vector.tensor_copy(gs[:], xs[:].indirect(offs_t[:]))
@@ -90,10 +93,9 @@ def tile_picked_swapgate_sigmoid_po_kernel(
             nc.vector.tensor_copy(dst[:].rearrange("p (t m) -> p m t", t=PACK), src[:].rearrange("p (m t) -> p m t", t=PACK))
 
         w2_c = sb("w2_c", [P, H], I32)
-        w3_c = sb("w3_c", [P, N], I32)
-        ws = keep.tile([P, H], U8, name="ws", tag="xw", align_bytes=64)
+        w2_s = keep.tile([P, H], U8, name="w2_s", tag="xw", align_bytes=64)
         deal(w2_c, w2_raw)
-        deal(ws, ws_raw)
+        deal(w2_s, w2s_raw)
 
         def mm(dst, lw, ls, t, rw, rs):
             cols = slice(P * t, P * t + P)
@@ -102,44 +104,42 @@ def tile_picked_swapgate_sigmoid_po_kernel(
             )
 
         y = [sb("y%d" % t, [P, S], F32) for t in range(PACK)]
-        pre = [sb("pre%d" % t, [P, S], F32) for t in range(PACK)]
         qq2 = [sb("qq%d" % u, [P, 2, 2, V], F32) for u in range(2)]
         order = (2, 0, 1, 3)
         qq = {t: qq2[i // 2][:, i % 2] for i, t in enumerate(order)}
-        a = [sb("a%d" % t, [P, V], F32) for t in range(PACK)]
+        a2 = [keep.tile([P, 2, V], F32, name="a%d" % u, tag=("w2_raw", "a1")[u], align_bytes=64) for u in range(2)]
+        a = {t: a2[i // 2][:, i % 2, :] for i, t in enumerate(order)}
         e = [sb("e%d" % t, [P, V], F32) for t in range(PACK)]
         df = [sb("df%d" % t, [P, 2, V], F32) for t in range(PACK)]
         z = [sb("z%d" % t, [P, S], F32) for t in range(PACK)]
         z_b = sb("z_b", [P, S, PACK], BF16)
 
-        def make_y(t, pieces):
-            width = S // pieces
-            for h in range(pieces):
-                cols = slice(width * h, width * h + width)
-                acc = bank([P, width])
-                mm(acc[:], w1_c[:], w1_s[:], t, gw[:, cols], gs[:, cols])
-                nc.scalar.copy(y[t][:, cols], acc[:])
+        def make_y(t, cols):
+            acc = bank([P, cols.stop - cols.start])
+            mm(acc[:], w1_c[:], w1_s[:], t, gw[:, cols], gs[:, cols])
+            nc.scalar.copy(y[t][:, cols], acc[:])
 
         def make_q(t):
             acc = bank([P, S])
-            mm(acc[:], w2_c[:], ws[:], t, gw[:], gs[:])
-            nc.scalar.copy(pre[t][:], acc[:])
-            nc.scalar.activation(qq[t][:, 0, :], pre[t][:].indirect(la_t[:]), ACT.Sigmoid)
+            mm(acc[:], w2_c[:], w2_s[:], t, gw[:], gs[:])
+            pre = keep.tile([P, S], F32, name="pre%d" % t, tag="pre%d" % min(order.index(t), 1), align_bytes=64)
+            nc.scalar.copy(pre[:], acc[:])
+            nc.scalar.activation(qq[t][:, 0, :], pre[:].indirect(la_t[:]), ACT.Sigmoid)
 
         def one_minus(both):
             nc.scalar.activation(both[:, :, 1, :], both[:, :, 0, :], ACT.Copy, bias=1.0, scale=-1.0)
 
         def get_a(t):
-            nc.vector.tensor_copy(a[t][:], y[t][:].indirect(la_t[:]))
+            nc.vector.tensor_copy(a[t], y[t][:].indirect(la_t[:]))
 
         def get_e(t):
-            nc.vector.tensor_tensor(e[t][:], y[t][:].indirect(lb_t[:]), a[t][:], ALU.subtract)
+            nc.vector.tensor_tensor(e[t][:], y[t][:].indirect(lb_t[:]), a[t], ALU.subtract)
 
         def get_df(t):
             nc.vector.tensor_tensor(df[t][:], qq[t], e[t][:].unsqueeze(1).to_broadcast([P, 2, V]), ALU.mult)
 
         def put(t, which):
-            nc.vector.tensor_tensor(z[t][:].indirect((la_t, lb_t)[which][:]), a[t][:], df[t][:, which, :], ALU.add)
+            nc.vector.tensor_tensor(z[t][:].indirect((la_t, lb_t)[which][:]), a[t], df[t][:, which, :], ALU.add)
 
         def weave(t):
             for c in range(0, S, CH):
@@ -149,37 +149,38 @@ def tile_picked_swapgate_sigmoid_po_kernel(
                     nc.scalar.copy(z_b[:, c : c + CH, t], z[t][:, c : c + CH])
 
         t0, t1, t2, t3 = order
-        make_y(t0, 2)
-        make_y(t1, 1)
-        make_q(t0)
-        one_minus(qq2[0][:, 0:1])
-        make_y(t2, 1)
-        make_q(t1)
-        one_minus(qq2[0][:, 1:2])
-        make_y(t3, 1)
-        make_q(t2)
-        make_q(t3)
-        one_minus(qq2[1][:])
-        get_a(t0)
-        deal(w3_c, w3_raw)
-        get_e(t0)
-        get_a(t1)
-        get_e(t1)
-        for i in range(2):
-            get_df(order[i])
-            get_a(order[i + 2])
-            put(order[i], 0)
-            get_e(order[i + 2])
-            put(order[i], 1)
-            weave(order[i])
-        get_df(t2)
-        get_df(t3)
-        put(t2, 0)
-        put(t3, 0)
-        put(t2, 1)
-        weave(t2)
-        put(t3, 1)
-        weave(t3)
+        for cols in (slice(0, S // 2), slice(S // 2, S)):
+            make_y(t0, cols)
+            make_y(t1, cols)
+        make_y(t2, slice(0, S))
+        make_y(t3, slice(0, S))
+        for u in range(2):
+            make_q(order[2 * u])
+            make_q(order[2 * u + 1])
+            one_minus(qq2[u][:])
+        for u in range(2):
+            pair = order[2 * u : 2 * u + 2]
+            for step in (get_a, get_e):
+                for t in pair:
+                    step(t)
+            if u == 0:
+                w3_c = keep.tile([P, N], I32, name="w3_c", tag="y%d" % t0, align_bytes=64)
+                deal(w3_c, w3_raw)
+        for u in range(2):
+            pair = order[2 * u : 2 * u + 2]
+            for t in pair:
+                get_df(t)
+            for which in range(2):
+                for t in pair:
+                    if which == 1 and t == t3:
+                        w3_s = keep.tile([P, N], U8, name="w3_s", tag="qq1", align_bytes=64)
+                        deal(w3_s, w3s_raw)
+                        idle = bank([P, S])
+                        for w in range(WARM):
+                            mm(idle[:], w3_c[:], w3_s[:], w, gw[:], gs[:])
+                    put(t, which)
+            for t in pair:
+                weave(t)
 
         z_c = sb("z_c", [P, S], U32)
         z_s = sb("z_s", [P, S], U8)
@@ -192,21 +193,28 @@ def tile_picked_swapgate_sigmoid_po_kernel(
         def quant(codes, scales, src, cols):
             nc.vector.quantize_mx(out=codes[:, cols].bitcast(FP8X4), scales=scales[:, cols], in_=src[:, cols, :].rearrange("p s t -> p (s t)"))
 
-        o = []
-        for i, cols in enumerate(chunks):
+        o_tiles = [sb("o0", [P, PACK, CH], F32), sb("o1", [P, PACK, CH], F32), sb("o23", [P, PACK, 2 * CH], F32)]
+        o = [o_tiles[0][:], o_tiles[1][:], o_tiles[2][:, :, 0:CH], o_tiles[2][:, :, CH : 2 * CH]]
+        for cols in chunks:
             quant(z_c, z_s, z_b, cols)
-            acc = bank([P, PACK, CH])
-            for t in range(PACK):
-                mm(acc[:, t, :], w3_c[:], ws[4:P, :], t, z_c[:, cols], z_s[:, cols])
-            o.append(sb("o%d" % i, [P, PACK, CH], F32))
-            nc.scalar.copy(o[i][:], acc[:])
-            nc.sync.dma_start(out_rows[:, :, cols], o[i][:])
+        accs = []
         for i, cols in enumerate(chunks):
-            nc.vector.tensor_copy(o_b[:, cols, :], o[i][:].rearrange("p t s -> p s t"))
+            accs.append(bank([P, PACK, CH]))
+            for t in range(PACK):
+                mm(accs[i][:, t, :], w3_c[:], w3_s[:], t, z_c[:, cols], z_s[:, cols])
+            if i == 1:
+                nc.vector.tensor_copy(o[i], accs[i][:])
+            else:
+                nc.scalar.copy(o[i], accs[i][:])
+            if i < 2:
+                nc.sync.dma_start(out_rows[:, :, cols], o[i])
+        nc.sync.dma_start(out_rows[:, :, 2 * CH : S], o_tiles[2][:])
+        for i, cols in enumerate(chunks[:3]):
+            nc.vector.tensor_copy(o_b[:, cols, :], o[i].rearrange("p t s -> p s t"))
+        nc.scalar.copy(o_b[:, chunks[3], :], accs[3][:].rearrange("p t s -> p s t"))
+        for cols in (slice(0, 2 * CH), chunks[2], chunks[3]):
             quant(o_c, o_s, o_b, cols)
-            if i % 2 == 1:
-                half = slice(CH * (i - 1), CH * (i + 1))
-                nc.sync.dma_start(words_of(out_1)[:, half], o_c[:, half].bitcast(I32))
-        for q in range(4):
-            queue = nc.scalar if q % 2 else nc.sync
-            queue.dma_start(out_2[0, 4 * q : 4 * q + 4, :].bitcast(I32), o_s[32 * q : 32 * q + 4, :].bitcast(I32))
+        nc.sync.dma_start(words_of(out_1), o_c[:].bitcast(I32))
+        for g in range(4):
+            queue = nc.scalar if g % 2 else nc.sync
+            queue.dma_start(out_2[0, 4 * g : 4 * g + 4, :].bitcast(I32), o_s[32 * g : 32 * g + 4, :].bitcast(I32))

@@ -44,8 +44,7 @@ def tile_picked_swapgate_sigmoid_po_kernel(
         lb_t = keep.tile([P, V // 16], U16, name="lb_t")
         xw = sb("xw", [P, T], U32)
         xs = sb("xs", [P, T], U8)
-        w2s_raw = sb("w2s_raw", [P, H], U8)
-        w3s_raw = sb("w3s_raw", [P, N], U8)
+        ws_raw = sb("ws_raw", [P, H], U8)
         w2_raw = sb("w2_raw", [P, H], I32)
         w3_raw = sb("w3_raw", [P, N], I32)
         w1_raw = [sb("w1_raw%d" % h, [P, PACK, H // 2], F32) for h in range(2)]
@@ -53,26 +52,25 @@ def tile_picked_swapgate_sigmoid_po_kernel(
         warm = sb("warm", [P, 2], F32)
         nc.vector.memset(xs[:].bitcast(I32), 0)
         nc.vector.memset(warm[:, 0:1], 0.0)
-        nc.gpsimd.memset(w2s_raw[:].bitcast(I32), 0)
-        nc.vector.memset(w3s_raw[:].bitcast(I32), 0)
+        nc.gpsimd.memset(ws_raw[:].bitcast(I32), 0)
         nc.scalar.activation(warm[:, 1:2], warm[:, 0:1], ACT.Sigmoid)
 
-        def load_scales(queue, dst, scales):
+        def load_scales(queue, dst, row, scales):
             for g in range(4):
-                queue.dma_start(dst[32 * g : 32 * g + 4, :].bitcast(I32), scales[0, 4 * g : 4 * g + 4, :].bitcast(I32))
+                queue.dma_start(dst[32 * g + row : 32 * g + row + 4, :].bitcast(I32), scales[0, 4 * g : 4 * g + 4, :].bitcast(I32))
 
         w1_rows = w1.rearrange("(p j) c -> p j c", j=PACK)
         nc.sync.dma_start(w1_raw[0][:], w1_rows[:, :, 0 : H // 2])
-        load_scales(nc.sync, xs, x_scales)
+        load_scales(nc.sync, xs, 0, x_scales)
         nc.sync.dma_start(offs_t[:], offs)
         nc.sync.dma_start(w1_raw[1][:], w1_rows[:, :, H // 2 : H])
         nc.sync.dma_start(xw[:].bitcast(I32), words_of(x_words))
         nc.sync.dma_start(la_t[:], la)
         nc.sync.dma_start(lb_t[:], lb)
         nc.sync.dma_start(w2_raw[:], words_of(w2_words))
-        load_scales(nc.gpsimd, w2s_raw, w2_scales)
+        load_scales(nc.gpsimd, ws_raw, 0, w2_scales)
+        load_scales(nc.sync, ws_raw, 4, w3_scales)
         nc.sync.dma_start(w3_raw[:], words_of(w3_words))
-        load_scales(nc.sync, w3s_raw, w3_scales)
 
         gs = sb("gs", [P, S], U8)
         nc.vector.tensor_copy(gs[:], xs[:].indirect(offs_t[:]))
@@ -89,13 +87,15 @@ def tile_picked_swapgate_sigmoid_po_kernel(
         for h in range(2):
             nc.vector.tensor_copy(gw[:, 256 * h : 256 * h + 256], xw[:].indirect(offs_t[:, 16 * h : 16 * h + 16]))
 
-        def deal(dst, src):
-            nc.vector.tensor_copy(dst[:].rearrange("p (t m) -> p m t", t=PACK), src[:].rearrange("p (m t) -> p m t", t=PACK))
+        def deal(dst, src, run):
+            nc.vector.tensor_copy(
+                dst[:].rearrange("p (t b i) -> p b t i", t=PACK, i=run), src[:].rearrange("p (b i t) -> p b t i", t=PACK, i=run)
+            )
 
         w2_c = sb("w2_c", [P, H], I32)
-        w2_s = keep.tile([P, H], U8, name="w2_s", tag="xw", align_bytes=64)
-        deal(w2_c, w2_raw)
-        deal(w2_s, w2s_raw)
+        ws = keep.tile([P, H], U8, name="ws", tag="xw", align_bytes=64)
+        deal(w2_c, w2_raw, 4)
+        deal(ws, ws_raw, 16)
 
         def mm(dst, lw, ls, t, rw, rs):
             cols = slice(P * t, P * t + P)
@@ -107,8 +107,8 @@ def tile_picked_swapgate_sigmoid_po_kernel(
         qq2 = [sb("qq%d" % u, [P, 2, 2, V], F32) for u in range(2)]
         order = (2, 0, 1, 3)
         qq = {t: qq2[i // 2][:, i % 2] for i, t in enumerate(order)}
-        a2 = [keep.tile([P, 2, V], F32, name="a%d" % u, tag=("w2_raw", "a1")[u], align_bytes=64) for u in range(2)]
-        a = {t: a2[i // 2][:, i % 2, :] for i, t in enumerate(order)}
+        a_all = keep.tile([P, PACK, V], F32, name="a_all", tag="ws_raw", align_bytes=64)
+        a = [a_all[:, t, :] for t in range(PACK)]
         e = [sb("e%d" % t, [P, V], F32) for t in range(PACK)]
         df = [sb("df%d" % t, [P, 2, V], F32) for t in range(PACK)]
         z = [sb("z%d" % t, [P, S], F32) for t in range(PACK)]
@@ -121,7 +121,7 @@ def tile_picked_swapgate_sigmoid_po_kernel(
 
         def make_q(t):
             acc = bank([P, S])
-            mm(acc[:], w2_c[:], w2_s[:], t, gw[:], gs[:])
+            mm(acc[:], w2_c[:], ws[:], t, gw[:], gs[:])
             pre = keep.tile([P, S], F32, name="pre%d" % t, tag="pre%d" % min(order.index(t), 1), align_bytes=64)
             nc.scalar.copy(pre[:], acc[:])
             nc.scalar.activation(qq[t][:, 0, :], pre[:].indirect(la_t[:]), ACT.Sigmoid)
@@ -163,9 +163,6 @@ def tile_picked_swapgate_sigmoid_po_kernel(
             for step in (get_a, get_e):
                 for t in pair:
                     step(t)
-            if u == 0:
-                w3_c = keep.tile([P, N], I32, name="w3_c", tag="y%d" % t0, align_bytes=64)
-                deal(w3_c, w3_raw)
         for u in range(2):
             pair = order[2 * u : 2 * u + 2]
             for t in pair:
@@ -173,11 +170,11 @@ def tile_picked_swapgate_sigmoid_po_kernel(
             for which in range(2):
                 for t in pair:
                     if which == 1 and t == t3:
-                        w3_s = keep.tile([P, N], U8, name="w3_s", tag="qq1", align_bytes=64)
-                        deal(w3_s, w3s_raw)
+                        w3_c = keep.tile([P, N], I32, name="w3_c", tag="qq1", align_bytes=64)
+                        deal(w3_c, w3_raw, 4)
                         idle = bank([P, S])
                         for w in range(WARM):
-                            mm(idle[:], w3_c[:], w3_s[:], w, gw[:], gs[:])
+                            mm(idle[:], w3_c[:], ws[4:P, :], w, gw[:], gs[:])
                     put(t, which)
             for t in pair:
                 weave(t)
@@ -201,7 +198,7 @@ def tile_picked_swapgate_sigmoid_po_kernel(
         for i, cols in enumerate(chunks):
             accs.append(bank([P, PACK, CH]))
             for t in range(PACK):
-                mm(accs[i][:, t, :], w3_c[:], w3_s[:], t, z_c[:, cols], z_s[:, cols])
+                mm(accs[i][:, t, :], w3_c[:], ws[4:P, :], t, z_c[:, cols], z_s[:, cols])
             if i == 1:
                 nc.vector.tensor_copy(o[i], accs[i][:])
             else:

@@ -1,6 +1,7 @@
 from contextlib import ExitStack
 
 import concourse.mybir as mybir
+from concourse.masks import make_identity
 
 K, T, S, V, N, H = 512, 2048, 512, 256, 512, 512
 FLOPS = 2 * K * H * S * 2 + 2 * H * N * S
@@ -103,81 +104,124 @@ def tile_picked_swapgate_sigmoid_po_kernel(
                 out=dst, lhsT=lw[:, cols].bitcast(FP8X4), lhsT_scale=ls[:, cols], rhs=rw.bitcast(FP8X4), rhs_scale=rs, start=True, stop=True
             )
 
-        y = [sb("y%d" % t, [P, S], F32) for t in range(PACK)]
-        qq2 = [sb("qq%d" % u, [P, 2, 2, V], F32) for u in range(2)]
+        ident = sb("ident", [P, P], F32)
+        make_identity(nc, ident[:])
+
         order = (2, 0, 1, 3)
-        qq = {t: qq2[i // 2][:, i % 2] for i, t in enumerate(order)}
-        a_all = keep.tile([P, PACK, V], F32, name="a_all", tag="ws_raw", align_bytes=64)
-        a = [a_all[:, t, :] for t in range(PACK)]
-        e = [sb("e%d" % t, [P, V], F32) for t in range(PACK)]
-        df = [sb("df%d" % t, [P, 2, V], F32) for t in range(PACK)]
-        z = [sb("z%d" % t, [P, S], F32) for t in range(PACK)]
+        y = [sb("y%d" % i, [P, S], F32) for i in range(PACK)]
+        pre = [sb("pre%d" % i, [P, S], F32) for i in range(PACK)]
+        q = sb("q", [P, PACK, V], F32)
+        a = keep.tile([P, PACK, V], F32, name="a", tag="ws_raw", align_bytes=64)
+        e = {}
+        turned = [sb("turned%d" % u, [P, 2 * V], F32) for u in range(2)]
+        b = [sb("b%d" % u, [P, 2, V], F32) for u in range(2)]
+        d = sb("d", [P, PACK, V], F32)
+        nd_tiles = [sb("nd0", [P, 1, V], F32), sb("nd12", [P, 2, V], F32), sb("nd3", [P, 1, V], F32)]
+        nd = [nd_tiles[0][:, 0, :], nd_tiles[1][:, 0, :], nd_tiles[1][:, 1, :], nd_tiles[2][:, 0, :]]
+        z = {}
         z_b = sb("z_b", [P, S, PACK], BF16)
 
-        def make_y(t, cols):
+        def make_y(i, cols):
             acc = bank([P, cols.stop - cols.start])
-            mm(acc[:], w1_c[:], w1_s[:], t, gw[:, cols], gs[:, cols])
-            nc.scalar.copy(y[t][:, cols], acc[:])
+            mm(acc[:], w1_c[:], w1_s[:], order[i], gw[:, cols], gs[:, cols])
+            nc.scalar.copy(y[i][:, cols], acc[:])
 
-        def make_q(t):
+        def make_pre(i):
             acc = bank([P, S])
-            mm(acc[:], w2_c[:], ws[:], t, gw[:], gs[:])
-            pre = keep.tile([P, S], F32, name="pre%d" % t, tag="pre%d" % min(order.index(t), 1), align_bytes=64)
-            nc.scalar.copy(pre[:], acc[:])
-            nc.scalar.activation(qq[t][:, 0, :], pre[:].indirect(la_t[:]), ACT.Sigmoid)
+            mm(acc[:], w2_c[:], ws[:], order[i], gw[:], gs[:])
+            nc.scalar.copy(pre[i][:], acc[:])
 
-        def one_minus(both):
-            nc.scalar.activation(both[:, :, 1, :], both[:, :, 0, :], ACT.Copy, bias=1.0, scale=-1.0)
+        def make_q(i):
+            nc.scalar.activation(q[:, i, :], pre[i][:].indirect(la_t[:]), ACT.Sigmoid)
 
-        def get_a(t):
-            nc.vector.tensor_copy(a[t], y[t][:].indirect(la_t[:]))
+        def get_a(i):
+            nc.vector.tensor_copy(a[:, i, :], y[i][:].indirect(la_t[:]))
 
-        def get_e(t):
-            nc.vector.tensor_tensor(e[t][:], y[t][:].indirect(lb_t[:]), a[t], ALU.subtract)
+        def get_e(i, tag):
+            e[i] = keep.tile([P, V], F32, name="e%d" % i, tag=tag, align_bytes=64)
+            nc.vector.tensor_tensor(e[i][:], y[i][:].indirect(lb_t[:]), a[:, i, :], ALU.subtract)
 
-        def get_df(t):
-            nc.vector.tensor_tensor(df[t][:], qq[t], e[t][:].unsqueeze(1).to_broadcast([P, 2, V]), ALU.mult)
+        def add_turned(u):
+            acc = bank([P, 2, V])
+            for h in range(2):
+                i = 2 * u + h
+                for c in range(0, V, P):
+                    nc.tensor.matmul(acc[:, h, c : c + P], a[:, i, c : c + P], ident[:], start=True, stop=False, is_transpose=True)
+                    nc.tensor.matmul(acc[:, h, c : c + P], e[i][:, c : c + P], ident[:], start=False, stop=True, is_transpose=True)
+            nc.scalar.copy(turned[u][:], acc[:].rearrange("p i v -> p (i v)"))
 
-        def put(t, which):
-            nc.vector.tensor_tensor(z[t][:].indirect((la_t, lb_t)[which][:]), a[t], df[t][:, which, :], ALU.add)
+        def turn_back(u):
+            acc = bank([P, 2 * V])
+            for c in range(0, 2 * V, P):
+                nc.tensor.transpose(acc[:, c : c + P], turned[u][:, c : c + P], ident[:])
+            nc.scalar.copy(b[u][:].rearrange("p i v -> p (i v)"), acc[:])
 
-        def weave(t):
+        def get_d(i):
+            nc.vector.tensor_tensor(d[:, i, :], q[:, i, :], e[i][:], ALU.mult)
+
+        def negate(k, planes):
+            nc.scalar.activation(nd_tiles[k][:], d[:, planes, :], ACT.Copy, scale=-1.0)
+
+        def put_a(i, tag):
+            z[i] = keep.tile([P, S], F32, name="z%d" % i, tag=tag, align_bytes=64)
+            nc.vector.tensor_tensor(z[i][:].indirect(la_t[:]), a[:, i, :], d[:, i, :], ALU.add)
+
+        def put_b(i):
+            nc.vector.tensor_tensor(z[i][:].indirect(lb_t[:]), b[i // 2][:, i % 2, :], nd[i], ALU.add)
+
+        def weave(i):
+            t = order[i]
             for c in range(0, S, CH):
                 if c == 0 and t >= 2:
-                    nc.vector.tensor_copy(z_b[:, c : c + CH, t], z[t][:, c : c + CH])
+                    nc.vector.tensor_copy(z_b[:, c : c + CH, t], z[i][:, c : c + CH])
                 else:
-                    nc.scalar.copy(z_b[:, c : c + CH, t], z[t][:, c : c + CH])
+                    nc.scalar.copy(z_b[:, c : c + CH, t], z[i][:, c : c + CH])
 
-        t0, t1, t2, t3 = order
         for cols in (slice(0, S // 2), slice(S // 2, S)):
-            make_y(t0, cols)
-            make_y(t1, cols)
-        make_y(t2, slice(0, S))
-        make_y(t3, slice(0, S))
-        for u in range(2):
-            make_q(order[2 * u])
-            make_q(order[2 * u + 1])
-            one_minus(qq2[u][:])
-        for u in range(2):
-            pair = order[2 * u : 2 * u + 2]
-            for step in (get_a, get_e):
-                for t in pair:
-                    step(t)
-        for u in range(2):
-            pair = order[2 * u : 2 * u + 2]
-            for t in pair:
-                get_df(t)
-            for which in range(2):
-                for t in pair:
-                    if which == 1 and t == t3:
-                        w3_c = keep.tile([P, N], I32, name="w3_c", tag="qq1", align_bytes=64)
-                        deal(w3_c, w3_raw, 4)
-                        idle = bank([P, S])
-                        for w in range(WARM):
-                            mm(idle[:], w3_c[:], ws[4:P, :], w, gw[:], gs[:])
-                    put(t, which)
-            for t in pair:
-                weave(t)
+            make_y(0, cols)
+            make_y(1, cols)
+        make_y(2, slice(0, S))
+        make_y(3, slice(0, S))
+        get_a(0)
+        get_a(1)
+        get_e(0, "e0")
+        get_e(1, "e1")
+        get_a(2)
+        get_a(3)
+        get_e(2, "e2")
+        for step in (make_pre, make_q):
+            step(0)
+            step(1)
+        get_d(0)
+        get_d(1)
+        get_e(3, "pre1")
+        put_a(0, "z0")
+        for step in (make_pre, make_q):
+            step(2)
+            step(3)
+        get_d(2)
+        get_d(3)
+        put_a(1, "pre3")
+        put_a(2, "pre2")
+        add_turned(0)
+        add_turned(1)
+        turn_back(0)
+        turn_back(1)
+        negate(0, slice(0, 1))
+        negate(1, slice(1, 3))
+        negate(2, slice(3, 4))
+        for i in range(3):
+            put_b(i)
+        for i in range(3):
+            weave(i)
+        put_a(3, "b0")
+        w3_c = keep.tile([P, N], I32, name="w3_c", tag="nd12", align_bytes=64)
+        deal(w3_c, w3_raw, 4)
+        idle = bank([P, S])
+        for w in range(WARM):
+            mm(idle[:], w3_c[:], ws[4:P, :], w, gw[:], gs[:])
+        put_b(3)
+        weave(3)
 
         z_c = sb("z_c", [P, S], U32)
         z_s = sb("z_s", [P, S], U8)

@@ -46,57 +46,77 @@ def tile_picked_swapgate_sigmoid_po_kernel(
         xw = sb("xw", [P, T], U32)
         xs = sb("xs", [P, T], U8)
         ws_raw = sb("ws_raw", [P, H], U8)
-        w2_raw = sb("w2_raw", [P, H], I32)
-        w3_raw = sb("w3_raw", [P, N], I32)
-        w1_raw = [sb("w1_raw%d" % h, [P, PACK, H // 2], F32) for h in range(2)]
+        w1_raw = [sb("w1_raw%d" % u, [P, 2, H], F32) for u in range(2)]
+        gs = sb("gs", [P, S], U8)
+        w2_s = sb("w2_s", [P, H], U8)
+        w3_s = sb("w3_s", [P, N], U8)
 
         warm = sb("warm", [P, 2], F32)
-        nc.vector.memset(xs[:].bitcast(I32), 0)
+        nc.gpsimd.memset(xs[0:96, :].bitcast(I32), 0)
+        nc.gpsimd.memset(xs[96:112, :].bitcast(I32), 0)
         nc.vector.memset(warm[:, 0:1], 0.0)
-        nc.gpsimd.memset(ws_raw[:].bitcast(I32), 0)
+        nc.vector.memset(ws_raw[0:96, :].bitcast(I32), 0)
+        nc.vector.memset(gs[:].bitcast(I32), 0)
+        nc.vector.memset(w2_s[:].bitcast(I32), 0)
+        nc.vector.memset(w3_s[:].bitcast(I32), 0)
         nc.scalar.activation(warm[:, 1:2], warm[:, 0:1], ACT.Sigmoid)
 
-        def load_scales(queue, dst, row, scales):
+        def place_scales(dst, src, first):
             for g in range(4):
-                queue.dma_start(dst[32 * g + row : 32 * g + row + 4, :].bitcast(I32), scales[0, 4 * g : 4 * g + 4, :].bitcast(I32))
+                nc.sync.dma_start(dst[32 * g : 32 * g + 4, :].bitcast(I32), src[first + 4 * g : first + 4 * g + 4, :].bitcast(I32))
 
         w1_rows = w1.rearrange("(p j) c -> p j c", j=PACK)
-        nc.sync.dma_start(w1_raw[0][:], w1_rows[:, :, 0 : H // 2])
-        load_scales(nc.sync, xs, 0, x_scales)
         nc.sync.dma_start(offs_t[:], offs)
-        nc.sync.dma_start(w1_raw[1][:], w1_rows[:, :, H // 2 : H])
+        nc.sync.dma_start(xs[112:P, :].bitcast(I32), x_scales[0].bitcast(I32))
         nc.sync.dma_start(xw[:].bitcast(I32), words_of(x_words))
+        nc.sync.dma_start(ws_raw[96:112, :].bitcast(I32), w2_scales[0].bitcast(I32))
+        nc.sync.dma_start(ws_raw[112:P, :].bitcast(I32), w3_scales[0].bitcast(I32))
+        for u in range(2):
+            nc.sync.dma_start(w1_raw[u][:], w1_rows[:, 2 * u : 2 * u + 2, :])
+        w2_raw = sb("w2_raw", [P, H], I32)
+        nc.sync.dma_start(w2_raw[:], words_of(w2_words))
         nc.sync.dma_start(la_t[:], la)
         nc.sync.dma_start(lb_t[:], lb)
-        nc.sync.dma_start(w2_raw[:], words_of(w2_words))
-        load_scales(nc.gpsimd, ws_raw, 0, w2_scales)
-        load_scales(nc.sync, ws_raw, 4, w3_scales)
-        nc.sync.dma_start(w3_raw[:], words_of(w3_words))
 
-        gs = sb("gs", [P, S], U8)
-        nc.vector.tensor_copy(gs[:], xs[:].indirect(offs_t[:]))
-
-        w1_b = sb("w1_b", [P, H * PACK], BF16)
-        w1_v = w1_b[:].rearrange("p (t m j) -> p m t j", t=PACK, j=PACK)
-        for h in range(2):
-            nc.vector.tensor_copy(w1_v[:, 64 * h : 64 * h + 64], w1_raw[h][:].rearrange("p j (m t) -> p m t j", t=PACK))
-        w1_c = sb("w1_c", [P, H], U32)
-        w1_s = sb("w1_s", [P, H], U8)
-        nc.vector.quantize_mx(out=w1_c[:].bitcast(FP8X4), scales=w1_s[:], in_=w1_b[:])
+        gs_raw = sb("gs_raw", [P, S], U8)
+        nc.vector.tensor_copy(gs_raw[:], xs[:].indirect(offs_t[:]))
+        place_scales(gs, gs_raw, 112)
 
         gw = sb("gw", [P, S], U32)
-        for h in range(2):
-            nc.vector.tensor_copy(gw[:, 256 * h : 256 * h + 256], xw[:].indirect(offs_t[:, 16 * h : 16 * h + 16]))
+        nc.vector.tensor_copy(gw[:], xw[:].indirect(offs_t[:]))
 
         def deal(dst, src, run):
             nc.vector.tensor_copy(
                 dst[:].rearrange("p (t b i) -> p b t i", t=PACK, i=run), src[:].rearrange("p (b i t) -> p b t i", t=PACK, i=run)
             )
 
+        ws_dealt = sb("ws_dealt", [P, H], U8)
+        deal(ws_dealt, ws_raw, 16)
+        place_scales(w2_s, ws_dealt, 96)
+        w3_raw = keep.tile([P, N], I32, name="w3_raw", tag="ws_raw", align_bytes=64)
+        nc.sync.dma_start(w3_raw[:], words_of(w3_words))
+        place_scales(w3_s, ws_dealt, 112)
+
+        order = (2, 0, 1, 3)
+        w1_b = sb("w1_b", [P, PACK, P, PACK], BF16)
+        w1_r = [w1_raw[u][:].rearrange("p j (m t) -> p t m j", t=PACK) for u in range(2)]
+        w1_c = sb("w1_c", [P, H], U32)
+        w1_s = sb("w1_s", [P, H], U8)
+
+        def quant_w1(t):
+            cols = slice(P * t, P * t + P)
+            nc.vector.quantize_mx(out=w1_c[:, cols].bitcast(FP8X4), scales=w1_s[:, cols], in_=w1_b[:, t].rearrange("p m j -> p (m j)"))
+
+        nc.vector.tensor_copy(w1_b[:, :, :, 0:2].rearrange("p t m j -> p m t j"), w1_r[0].rearrange("p t m j -> p m t j"))
+        for t in order[:2]:
+            nc.vector.tensor_copy(w1_b[:, t, :, 2:PACK], w1_r[1][:, t])
+        for t in order[2:]:
+            nc.scalar.copy(w1_b[:, t, :, 2:PACK], w1_r[1][:, t])
+        for t in order:
+            quant_w1(t)
+
         w2_c = sb("w2_c", [P, H], I32)
-        ws = keep.tile([P, H], U8, name="ws", tag="xw", align_bytes=64)
         deal(w2_c, w2_raw, 4)
-        deal(ws, ws_raw, 16)
 
         def mm(dst, lw, ls, t, rw, rs):
             cols = slice(P * t, P * t + P)
@@ -107,11 +127,10 @@ def tile_picked_swapgate_sigmoid_po_kernel(
         ident = sb("ident", [P, P], F32)
         make_identity(nc, ident[:])
 
-        order = (2, 0, 1, 3)
         y = [sb("y%d" % i, [P, S], F32) for i in range(PACK)]
         pre = [sb("pre%d" % i, [P, S], F32) for i in range(PACK)]
         q = sb("q", [P, PACK, V], F32)
-        a = keep.tile([P, PACK, V], F32, name="a", tag="ws_raw", align_bytes=64)
+        a = keep.tile([P, PACK, V], F32, name="a", tag="w2_raw", align_bytes=64)
         e = {}
         turned = [sb("turned%d" % u, [P, 2 * V], F32) for u in range(2)]
         b = [sb("b%d" % u, [P, 2, V], F32) for u in range(2)]
@@ -121,25 +140,33 @@ def tile_picked_swapgate_sigmoid_po_kernel(
         z = {}
         z_b = sb("z_b", [P, S, PACK], BF16)
 
-        def make_y(i, cols):
+        def make_y(i, cols, copy):
             acc = bank([P, cols.stop - cols.start])
             mm(acc[:], w1_c[:], w1_s[:], order[i], gw[:, cols], gs[:, cols])
-            nc.scalar.copy(y[i][:, cols], acc[:])
+            copy(y[i][:, cols], acc[:])
+
+        gate_banks = {}
+
+        def multiply_gate(i):
+            gate_banks[i] = bank([P, S])
+            mm(gate_banks[i][:], w2_c[:], w2_s[:], order[i], gw[:], gs[:])
 
         def make_pre(i):
-            acc = bank([P, S])
-            mm(acc[:], w2_c[:], ws[:], order[i], gw[:], gs[:])
-            nc.scalar.copy(pre[i][:], acc[:])
+            nc.scalar.copy(pre[i][:], gate_banks[i][:])
 
         def make_q(i):
             nc.scalar.activation(q[:, i, :], pre[i][:].indirect(la_t[:]), ACT.Sigmoid)
 
-        def get_a(i):
-            nc.vector.tensor_copy(a[:, i, :], y[i][:].indirect(la_t[:]))
+        def get_a(i, pieces=1):
+            n = V // pieces
+            for v in range(0, V, n):
+                nc.vector.tensor_copy(a[:, i, v : v + n], y[i][:].indirect(la_t[:, v // 16 : (v + n) // 16]))
 
-        def get_e(i, tag):
+        def get_e(i, tag, pieces=1):
             e[i] = keep.tile([P, V], F32, name="e%d" % i, tag=tag, align_bytes=64)
-            nc.vector.tensor_tensor(e[i][:], y[i][:].indirect(lb_t[:]), a[:, i, :], ALU.subtract)
+            n = V // pieces
+            for v in range(0, V, n):
+                nc.vector.tensor_tensor(e[i][:, v : v + n], y[i][:].indirect(lb_t[:, v // 16 : (v + n) // 16]), a[:, i, v : v + n], ALU.subtract)
 
         def add_turned(u):
             acc = bank([P, 2, V])
@@ -177,18 +204,22 @@ def tile_picked_swapgate_sigmoid_po_kernel(
                 else:
                     nc.scalar.copy(z_b[:, c : c + CH, t], z[i][:, c : c + CH])
 
-        for cols in (slice(0, S // 2), slice(S // 2, S)):
-            make_y(0, cols)
-            make_y(1, cols)
-        make_y(2, slice(0, S))
-        make_y(3, slice(0, S))
-        get_a(0)
+        halves = (slice(0, S // 2), slice(S // 2, S))
+        make_y(0, halves[0], nc.scalar.copy)
+        make_y(0, halves[1], nc.vector.tensor_copy)
+        make_y(1, halves[0], nc.scalar.copy)
+        make_y(1, halves[1], nc.scalar.copy)
+        make_y(2, slice(0, S), nc.scalar.copy)
+        make_y(3, slice(0, S), nc.scalar.copy)
+        for i in range(PACK):
+            multiply_gate(i)
+        get_a(0, 2)
+        get_e(0, "e0", 2)
         get_a(1)
-        get_e(0, "e0")
-        get_e(1, "e1")
         get_a(2)
+        get_e(1, "w1_s")
         get_a(3)
-        get_e(2, "e2")
+        get_e(2, "w2_s")
         for step in (make_pre, make_q):
             step(0)
             step(1)
@@ -219,7 +250,7 @@ def tile_picked_swapgate_sigmoid_po_kernel(
         deal(w3_c, w3_raw, 4)
         idle = bank([P, S])
         for w in range(WARM):
-            mm(idle[:], w3_c[:], ws[4:P, :], w, gw[:], gs[:])
+            mm(idle[:], w3_c[:], w3_s[:], w, gw[:], gs[:])
         put_b(3)
         weave(3)
 
@@ -242,7 +273,7 @@ def tile_picked_swapgate_sigmoid_po_kernel(
         for i, cols in enumerate(chunks):
             accs.append(bank([P, PACK, CH]))
             for t in range(PACK):
-                mm(accs[i][:, t, :], w3_c[:], ws[4:P, :], t, z_c[:, cols], z_s[:, cols])
+                mm(accs[i][:, t, :], w3_c[:], w3_s[:], t, z_c[:, cols], z_s[:, cols])
             if i == 1:
                 nc.vector.tensor_copy(o[i], accs[i][:])
             else:

@@ -135,8 +135,7 @@ def tile_picked_swapgate_sigmoid_po_kernel(
         turned = [sb("turned%d" % u, [P, 2 * V], F32) for u in range(2)]
         b = [sb("b%d" % u, [P, 2, V], F32) for u in range(2)]
         d = sb("d", [P, PACK, V], F32)
-        nd_tiles = [sb("nd0", [P, 1, V], F32), sb("nd12", [P, 2, V], F32), sb("nd3", [P, 1, V], F32)]
-        nd = [nd_tiles[0][:, 0, :], nd_tiles[1][:, 0, :], nd_tiles[1][:, 1, :], nd_tiles[2][:, 0, :]]
+        nd = {}
         z = {}
         z_b = sb("z_b", [P, S, PACK], BF16)
 
@@ -186,15 +185,16 @@ def tile_picked_swapgate_sigmoid_po_kernel(
         def get_d(i):
             nc.vector.tensor_tensor(d[:, i, :], q[:, i, :], e[i][:], ALU.mult)
 
-        def negate(k, planes):
-            nc.scalar.activation(nd_tiles[k][:], d[:, planes, :], ACT.Copy, scale=-1.0)
+        def negate(i, tag):
+            nd[i] = keep.tile([P, V], F32, name="nd%d" % i, tag=tag, align_bytes=64)
+            nc.scalar.activation(nd[i][:], d[:, i, :], ACT.Copy, scale=-1.0)
 
         def put_a(i, tag):
             z[i] = keep.tile([P, S], F32, name="z%d" % i, tag=tag, align_bytes=64)
             nc.vector.tensor_tensor(z[i][:].indirect(la_t[:]), a[:, i, :], d[:, i, :], ALU.add)
 
         def put_b(i):
-            nc.vector.tensor_tensor(z[i][:].indirect(lb_t[:]), b[i // 2][:, i % 2, :], nd[i], ALU.add)
+            nc.vector.tensor_tensor(z[i][:].indirect(lb_t[:]), b[i // 2][:, i % 2, :], nd[i][:], ALU.add)
 
         def weave(i):
             t = order[i]
@@ -234,19 +234,19 @@ def tile_picked_swapgate_sigmoid_po_kernel(
         get_d(3)
         put_a(1, "pre3")
         put_a(2, "pre2")
+        put_a(3, "z3")
         add_turned(0)
         add_turned(1)
+        for i in range(3):
+            negate(i, "nd%d" % i)
         turn_back(0)
         turn_back(1)
-        negate(0, slice(0, 1))
-        negate(1, slice(1, 3))
-        negate(2, slice(3, 4))
+        negate(3, "turned1")
         for i in range(3):
             put_b(i)
         for i in range(3):
             weave(i)
-        put_a(3, "b0")
-        w3_c = keep.tile([P, N], I32, name="w3_c", tag="nd12", align_bytes=64)
+        w3_c = keep.tile([P, N], I32, name="w3_c", tag="b0", align_bytes=64)
         deal(w3_c, w3_raw, 4)
         idle = bank([P, S])
         for w in range(WARM):

@@ -97,7 +97,7 @@ def tile_picked_swapgate_sigmoid_po_kernel(
         nc.sync.dma_start(w3_raw[:], words_of(w3_words))
         place_scales(w3_s, ws_dealt, 112)
 
-        order = (2, 0, 1, 3)
+        order = (1, 3, 0, 2)
         w1_b = sb("w1_b", [P, PACK, P, PACK], BF16)
         w1_r = [w1_raw[u][:].rearrange("p j (m t) -> p t m j", t=PACK) for u in range(2)]
         w1_c = sb("w1_c", [P, H], U32)
@@ -107,7 +107,8 @@ def tile_picked_swapgate_sigmoid_po_kernel(
             cols = slice(P * t, P * t + P)
             nc.vector.quantize_mx(out=w1_c[:, cols].bitcast(FP8X4), scales=w1_s[:, cols], in_=w1_b[:, t].rearrange("p m j -> p (m j)"))
 
-        nc.vector.tensor_copy(w1_b[:, :, :, 0:2].rearrange("p t m j -> p m t j"), w1_r[0].rearrange("p t m j -> p m t j"))
+        for copy, ms in ((nc.vector.tensor_copy, slice(0, 80)), (nc.scalar.copy, slice(80, P))):
+            copy(w1_b[:, :, ms, 0:2].rearrange("p t m j -> p m t j"), w1_r[0][:, :, ms].rearrange("p t m j -> p m t j"))
         for t in order[:2]:
             nc.vector.tensor_copy(w1_b[:, t, :, 2:PACK], w1_r[1][:, t])
         for t in order[2:]:
@@ -190,19 +191,17 @@ def tile_picked_swapgate_sigmoid_po_kernel(
             nc.scalar.activation(nd[i][:], d[:, i, :], ACT.Copy, scale=-1.0)
 
         def put_a(i, tag):
-            z[i] = keep.tile([P, S], F32, name="z%d" % i, tag=tag, align_bytes=64)
+            z[i] = keep.tile([P, S if i < 2 else 2 * S], F32, name="z%d" % i, tag=tag, align_bytes=64)
             nc.vector.tensor_tensor(z[i][:].indirect(la_t[:]), a[:, i, :], d[:, i, :], ALU.add)
 
         def put_b(i):
             nc.vector.tensor_tensor(z[i][:].indirect(lb_t[:]), b[i // 2][:, i % 2, :], nd[i][:], ALU.add)
 
-        def weave(i):
-            t = order[i]
-            for c in range(0, S, CH):
-                if c == 0 and t >= 2:
-                    nc.vector.tensor_copy(z_b[:, c : c + CH, t], z[i][:, c : c + CH])
-                else:
-                    nc.scalar.copy(z_b[:, c : c + CH, t], z[i][:, c : c + CH])
+        def weave(i, copies):
+            n = S // len(copies)
+            pair = z[i][:].rearrange("p (r s) -> p s r", r=2)
+            for c, copy in enumerate(copies):
+                copy(z_b[:, n * c : n * c + n, order[i] : order[i] + 2], pair[:, n * c : n * c + n, :])
 
         halves = (slice(0, S // 2), slice(S // 2, S))
         make_y(0, halves[0], nc.scalar.copy)
@@ -241,52 +240,62 @@ def tile_picked_swapgate_sigmoid_po_kernel(
             negate(i, "nd%d" % i)
         turn_back(0)
         turn_back(1)
-        negate(3, "turned1")
-        for i in range(3):
+        negate(3, "nd3")
+        for i in range(2):
             put_b(i)
-        for i in range(3):
-            weave(i)
-        w3_c = keep.tile([P, N], I32, name="w3_c", tag="b0", align_bytes=64)
+            nc.scalar.copy(z[i + 2][:, S : 2 * S], z[i][:])
+        put_b(2)
+        weave(2, [nc.scalar.copy] * 2)
+        w3_c = keep.tile([P, N], I32, name="w3_c", tag="z0", align_bytes=64)
         deal(w3_c, w3_raw, 4)
         idle = bank([P, S])
         for w in range(WARM):
             mm(idle[:], w3_c[:], w3_s[:], w, gw[:], gs[:])
         put_b(3)
-        weave(3)
+        weave(3, [nc.vector.tensor_copy] * 2 + [nc.scalar.copy] * 2)
 
-        z_c = sb("z_c", [P, S], U32)
         z_s = sb("z_s", [P, S], U8)
         o_b = sb("o_b", [P, S, PACK], BF16)
         o_c = sb("o_c", [P, S], U32)
         o_s = sb("o_s", [P, S], U8)
         out_rows = out_0.rearrange("(p t) s -> p t s", t=PACK)
+        out_words = words_of(out_1)
         chunks = [slice(c, c + CH) for c in range(0, S, CH)]
 
-        def quant(codes, scales, src, cols):
-            nc.vector.quantize_mx(out=codes[:, cols].bitcast(FP8X4), scales=scales[:, cols], in_=src[:, cols, :].rearrange("p s t -> p (s t)"))
+        def quant(codes, scales, src):
+            nc.vector.quantize_mx(out=codes.bitcast(FP8X4), scales=scales, in_=src.rearrange("p s t -> p (s t)"))
 
         o_tiles = [sb("o0", [P, PACK, CH], F32), sb("o1", [P, PACK, CH], F32), sb("o23", [P, PACK, 2 * CH], F32)]
         o = [o_tiles[0][:], o_tiles[1][:], o_tiles[2][:, :, 0:CH], o_tiles[2][:, :, CH : 2 * CH]]
-        for cols in chunks:
-            quant(z_c, z_s, z_b, cols)
-        accs = []
-        for i, cols in enumerate(chunks):
-            accs.append(bank([P, PACK, CH]))
+        accs = {}
+        z_c = {}
+
+        def quant_z(c):
+            z_c[c] = keep.tile([P, CH], U32, name="z_c%d" % c, tag="z_c%d" % (c % 3), align_bytes=64)
+            quant(z_c[c][:], z_s[:, chunks[c]], z_b[:, chunks[c], :])
+
+        def last_layer(c, copy):
+            accs[c] = bank([P, PACK, CH])
             for t in range(PACK):
-                mm(accs[i][:, t, :], w3_c[:], w3_s[:], t, z_c[:, cols], z_s[:, cols])
-            if i == 1:
-                nc.vector.tensor_copy(o[i], accs[i][:])
-            else:
-                nc.scalar.copy(o[i], accs[i][:])
-            if i < 2:
-                nc.sync.dma_start(out_rows[:, :, cols], o[i])
+                mm(accs[c][:, t, :], w3_c[:], w3_s[:], t, z_c[c][:], z_s[:, chunks[c]])
+            copy(o[c], accs[c][:])
+            if c < 2:
+                nc.sync.dma_start(out_rows[:, :, chunks[c]], o[c])
+
+        for c in range(3):
+            quant_z(c)
+        last_layer(0, nc.vector.tensor_copy)
+        quant_z(3)
+        for c in range(1, 4):
+            last_layer(c, nc.scalar.copy)
         nc.sync.dma_start(out_rows[:, :, 2 * CH : S], o_tiles[2][:])
-        for i, cols in enumerate(chunks[:3]):
-            nc.vector.tensor_copy(o_b[:, cols, :], o[i].rearrange("p t s -> p s t"))
+        for c in range(3):
+            nc.vector.tensor_copy(o_b[:, chunks[c], :], o[c].rearrange("p t s -> p s t"))
         nc.scalar.copy(o_b[:, chunks[3], :], accs[3][:].rearrange("p t s -> p s t"))
-        for cols in (slice(0, 2 * CH), chunks[2], chunks[3]):
-            quant(o_c, o_s, o_b, cols)
-        nc.sync.dma_start(words_of(out_1), o_c[:].bitcast(I32))
+        for cols in (halves[0], chunks[2], chunks[3]):
+            quant(o_c[:, cols], o_s[:, cols], o_b[:, cols, :])
+        for cols in halves:
+            nc.sync.dma_start(out_words[:, cols], o_c[:, cols].bitcast(I32))
         for g in range(4):
             queue = nc.scalar if g % 2 else nc.sync
             queue.dma_start(out_2[0, 4 * g : 4 * g + 4, :].bitcast(I32), o_s[32 * g : 32 * g + 4, :].bitcast(I32))

@@ -268,26 +268,17 @@ def tile_picked_swapgate_sigmoid_po_kernel(
         o_tiles = [sb("o0", [P, PACK, CH], F32), sb("o1", [P, PACK, CH], F32), sb("o23", [P, PACK, 2 * CH], F32)]
         o = [o_tiles[0][:], o_tiles[1][:], o_tiles[2][:, :, 0:CH], o_tiles[2][:, :, CH : 2 * CH]]
         accs = {}
-        z_c = {}
-
-        def quant_z(c):
-            z_c[c] = keep.tile([P, CH], U32, name="z_c%d" % c, tag="z_c%d" % (c % 3), align_bytes=64)
-            quant(z_c[c][:], z_s[:, chunks[c]], z_b[:, chunks[c], :])
-
-        def last_layer(c, copy):
+        z_c = sb("z_c", [P, S], U32)
+        for cols in chunks:
+            quant(z_c[:, cols], z_s[:, cols], z_b[:, cols, :])
+        for c, cols in enumerate(chunks):
             accs[c] = bank([P, PACK, CH])
             for t in range(PACK):
-                mm(accs[c][:, t, :], w3_c[:], w3_s[:], t, z_c[c][:], z_s[:, chunks[c]])
+                mm(accs[c][:, t, :], w3_c[:], w3_s[:], t, z_c[:, cols], z_s[:, cols])
+            copy = nc.vector.tensor_copy if c == 1 else nc.scalar.copy
             copy(o[c], accs[c][:])
             if c < 2:
-                nc.sync.dma_start(out_rows[:, :, chunks[c]], o[c])
-
-        for c in range(3):
-            quant_z(c)
-        last_layer(0, nc.vector.tensor_copy)
-        quant_z(3)
-        for c in range(1, 4):
-            last_layer(c, nc.scalar.copy)
+                nc.sync.dma_start(out_rows[:, :, cols], o[c])
         nc.sync.dma_start(out_rows[:, :, 2 * CH : S], o_tiles[2][:])
         for c in range(3):
             nc.vector.tensor_copy(o_b[:, chunks[c], :], o[c].rearrange("p t s -> p s t"))

@@ -18,8 +18,17 @@ ACT = mybir.ActivationFunctionType
 
 P = 128
 PACK = 4
-CH = 128
-WARM = 3
+CHUNK = 128
+LIST = 16
+BLOCKS = 16
+UPPER = P - BLOCKS
+LOWER = P - 2 * BLOCKS
+LINE_WORDS = 4
+LINE_BYTES = 16
+VECTOR_SHARE = 80
+WARM_PASSES = 3
+
+PLANE = (1, 3, 0, 2)
 
 
 def words_of(packed):
@@ -34,15 +43,15 @@ def tile_picked_swapgate_sigmoid_po_kernel(
         keep = ctx.enter_context(tc.tile_pool(name="keep", bufs=1))
         psum = ctx.enter_context(tc.psum_pool(name="psum", bufs=8))
 
-        def sb(name, shape, dtype):
-            return keep.tile(shape, dtype, name=name, align_bytes=64)
+        def sb(name, shape, dtype, reuses=None):
+            return keep.tile(shape, dtype, name=name, tag=reuses or name, align_bytes=64)
 
         def bank(shape):
             return psum.tile(shape, F32, name="bank")
 
-        offs_t = keep.tile([P, S // 16], U16, name="offs_t")
-        la_t = keep.tile([P, V // 16], U16, name="la_t")
-        lb_t = keep.tile([P, V // 16], U16, name="lb_t")
+        offs_t = keep.tile([P, S // LIST], U16, name="offs_t")
+        la_t = keep.tile([P, V // LIST], U16, name="la_t")
+        lb_t = keep.tile([P, V // LIST], U16, name="lb_t")
         xw = sb("xw", [P, T], U32)
         xs = sb("xs", [P, T], U8)
         ws_raw = sb("ws_raw", [P, H], U8)
@@ -52,10 +61,10 @@ def tile_picked_swapgate_sigmoid_po_kernel(
         w3_s = sb("w3_s", [P, N], U8)
 
         warm = sb("warm", [P, 2], F32)
-        nc.gpsimd.memset(xs[0:96, :].bitcast(I32), 0)
-        nc.gpsimd.memset(xs[96:112, :].bitcast(I32), 0)
+        nc.gpsimd.memset(xs[0:LOWER, :].bitcast(I32), 0)
+        nc.gpsimd.memset(xs[LOWER:UPPER, :].bitcast(I32), 0)
         nc.vector.memset(warm[:, 0:1], 0.0)
-        nc.vector.memset(ws_raw[0:96, :].bitcast(I32), 0)
+        nc.vector.memset(ws_raw[0:LOWER, :].bitcast(I32), 0)
         nc.vector.memset(gs[:].bitcast(I32), 0)
         nc.vector.memset(w2_s[:].bitcast(I32), 0)
         nc.vector.memset(w3_s[:].bitcast(I32), 0)
@@ -67,20 +76,20 @@ def tile_picked_swapgate_sigmoid_po_kernel(
 
         w1_rows = w1.rearrange("(p j) c -> p j c", j=PACK)
         nc.sync.dma_start(offs_t[:], offs)
-        nc.sync.dma_start(xs[112:P, :].bitcast(I32), x_scales[0].bitcast(I32))
+        nc.scalar.dma_start(xs[UPPER:P, :].bitcast(I32), x_scales[0].bitcast(I32))
         nc.sync.dma_start(xw[:].bitcast(I32), words_of(x_words))
-        nc.sync.dma_start(ws_raw[96:112, :].bitcast(I32), w2_scales[0].bitcast(I32))
-        nc.sync.dma_start(ws_raw[112:P, :].bitcast(I32), w3_scales[0].bitcast(I32))
+        nc.sync.dma_start(ws_raw[LOWER:UPPER, :].bitcast(I32), w2_scales[0].bitcast(I32))
+        nc.sync.dma_start(ws_raw[UPPER:P, :].bitcast(I32), w3_scales[0].bitcast(I32))
         for u in range(2):
             nc.sync.dma_start(w1_raw[u][:], w1_rows[:, 2 * u : 2 * u + 2, :])
-        w2_raw = sb("w2_raw", [P, H], I32)
-        nc.sync.dma_start(w2_raw[:], words_of(w2_words))
         nc.sync.dma_start(la_t[:], la)
         nc.sync.dma_start(lb_t[:], lb)
 
         gs_raw = sb("gs_raw", [P, S], U8)
         nc.vector.tensor_copy(gs_raw[:], xs[:].indirect(offs_t[:]))
-        place_scales(gs, gs_raw, 112)
+        place_scales(gs, gs_raw, UPPER)
+        w2_raw = sb("w2_raw", [P, H], I32, reuses="xs")
+        nc.sync.dma_start(w2_raw[:], words_of(w2_words))
 
         gw = sb("gw", [P, S], U32)
         nc.vector.tensor_copy(gw[:], xw[:].indirect(offs_t[:]))
@@ -91,38 +100,44 @@ def tile_picked_swapgate_sigmoid_po_kernel(
             )
 
         ws_dealt = sb("ws_dealt", [P, H], U8)
-        deal(ws_dealt, ws_raw, 16)
-        place_scales(w2_s, ws_dealt, 96)
-        w3_raw = keep.tile([P, N], I32, name="w3_raw", tag="ws_raw", align_bytes=64)
+        deal(ws_dealt, ws_raw, LINE_BYTES)
+        place_scales(w2_s, ws_dealt, LOWER)
+        w3_raw = sb("w3_raw", [P, N], I32, reuses="ws_raw")
         nc.sync.dma_start(w3_raw[:], words_of(w3_words))
-        place_scales(w3_s, ws_dealt, 112)
+        place_scales(w3_s, ws_dealt, UPPER)
 
-        order = (1, 3, 0, 2)
         w1_b = sb("w1_b", [P, PACK, P, PACK], BF16)
         w1_r = [w1_raw[u][:].rearrange("p j (m t) -> p t m j", t=PACK) for u in range(2)]
         w1_c = sb("w1_c", [P, H], U32)
         w1_s = sb("w1_s", [P, H], U8)
 
-        def quant_w1(t):
-            cols = slice(P * t, P * t + P)
-            nc.vector.quantize_mx(out=w1_c[:, cols].bitcast(FP8X4), scales=w1_s[:, cols], in_=w1_b[:, t].rearrange("p m j -> p (m j)"))
+        def quant(codes, scales, src):
+            nc.vector.quantize_mx(out=codes.bitcast(FP8X4), scales=scales, in_=src.rearrange("p s t -> p (s t)"))
 
-        for copy, ms in ((nc.vector.tensor_copy, slice(0, 80)), (nc.scalar.copy, slice(80, P))):
+        def plane_cols(t):
+            return slice(P * t, P * t + P)
+
+        for copy, ms in ((nc.vector.tensor_copy, slice(0, VECTOR_SHARE)), (nc.scalar.copy, slice(VECTOR_SHARE, P))):
             copy(w1_b[:, :, ms, 0:2].rearrange("p t m j -> p m t j"), w1_r[0][:, :, ms].rearrange("p t m j -> p m t j"))
-        for t in order[:2]:
-            nc.vector.tensor_copy(w1_b[:, t, :, 2:PACK], w1_r[1][:, t])
-        for t in order[2:]:
+        for copy, ms in ((nc.vector.tensor_copy, slice(0, P // 2)), (nc.scalar.copy, slice(P // 2, P))):
+            copy(w1_b[:, PLANE[0], ms, 2:PACK], w1_r[1][:, PLANE[0], ms])
+        nc.vector.tensor_copy(w1_b[:, PLANE[1], :, 2:PACK], w1_r[1][:, PLANE[1]])
+        for t in PLANE[2:]:
             nc.scalar.copy(w1_b[:, t, :, 2:PACK], w1_r[1][:, t])
-        for t in order:
-            quant_w1(t)
+        for t in PLANE:
+            quant(w1_c[:, plane_cols(t)], w1_s[:, plane_cols(t)], w1_b[:, t])
 
         w2_c = sb("w2_c", [P, H], I32)
-        deal(w2_c, w2_raw, 4)
 
-        def mm(dst, lw, ls, t, rw, rs):
-            cols = slice(P * t, P * t + P)
+        def mm(dst, weights, weight_scales, moving, moving_scales):
             nc.tensor.matmul_mx(
-                out=dst, lhsT=lw[:, cols].bitcast(FP8X4), lhsT_scale=ls[:, cols], rhs=rw.bitcast(FP8X4), rhs_scale=rs, start=True, stop=True
+                out=dst,
+                lhsT=weights.bitcast(FP8X4),
+                lhsT_scale=weight_scales,
+                rhs=moving.bitcast(FP8X4),
+                rhs_scale=moving_scales,
+                start=True,
+                stop=True,
             )
 
         ident = sb("ident", [P, P], F32)
@@ -131,42 +146,42 @@ def tile_picked_swapgate_sigmoid_po_kernel(
         y = [sb("y%d" % i, [P, S], F32) for i in range(PACK)]
         pre = [sb("pre%d" % i, [P, S], F32) for i in range(PACK)]
         q = sb("q", [P, PACK, V], F32)
-        a = keep.tile([P, PACK, V], F32, name="a", tag="w2_raw", align_bytes=64)
+        a = sb("a", [P, PACK, V], F32)
         e = {}
-        turned = [sb("turned%d" % u, [P, 2 * V], F32) for u in range(2)]
+        b_turned = [sb("b_turned%d" % u, [P, 2 * V], F32) for u in range(2)]
         b = [sb("b%d" % u, [P, 2, V], F32) for u in range(2)]
         d = sb("d", [P, PACK, V], F32)
-        nd = {}
+        minus_d = {}
         z = {}
         z_b = sb("z_b", [P, S, PACK], BF16)
+        gate_banks = {}
 
         def make_y(i, cols, copy):
             acc = bank([P, cols.stop - cols.start])
-            mm(acc[:], w1_c[:], w1_s[:], order[i], gw[:, cols], gs[:, cols])
+            mm(acc[:], w1_c[:, plane_cols(PLANE[i])], w1_s[:, plane_cols(PLANE[i])], gw[:, cols], gs[:, cols])
             copy(y[i][:, cols], acc[:])
-
-        gate_banks = {}
 
         def multiply_gate(i):
             gate_banks[i] = bank([P, S])
-            mm(gate_banks[i][:], w2_c[:], w2_s[:], order[i], gw[:], gs[:])
+            mm(gate_banks[i][:], w2_c[:, plane_cols(PLANE[i])], w2_s[:, plane_cols(PLANE[i])], gw[:], gs[:])
 
-        def make_pre(i):
+        def copy_gate(i):
             nc.scalar.copy(pre[i][:], gate_banks[i][:])
 
-        def make_q(i):
+        def get_q(i):
             nc.scalar.activation(q[:, i, :], pre[i][:].indirect(la_t[:]), ACT.Sigmoid)
 
         def get_a(i, pieces=1):
             n = V // pieces
             for v in range(0, V, n):
-                nc.vector.tensor_copy(a[:, i, v : v + n], y[i][:].indirect(la_t[:, v // 16 : (v + n) // 16]))
+                nc.vector.tensor_copy(a[:, i, v : v + n], y[i][:].indirect(la_t[:, v // LIST : (v + n) // LIST]))
 
-        def get_e(i, tag, pieces=1):
-            e[i] = keep.tile([P, V], F32, name="e%d" % i, tag=tag, align_bytes=64)
+        def get_e(i, reuses=None, pieces=1):
+            e[i] = sb("e%d" % i, [P, V], F32, reuses)
             n = V // pieces
             for v in range(0, V, n):
-                nc.vector.tensor_tensor(e[i][:, v : v + n], y[i][:].indirect(lb_t[:, v // 16 : (v + n) // 16]), a[:, i, v : v + n], ALU.subtract)
+                window = y[i][:].indirect(lb_t[:, v // LIST : (v + n) // LIST])
+                nc.vector.tensor_tensor(e[i][:, v : v + n], window, a[:, i, v : v + n], ALU.subtract)
 
         def add_turned(u):
             acc = bank([P, 2, V])
@@ -175,83 +190,91 @@ def tile_picked_swapgate_sigmoid_po_kernel(
                 for c in range(0, V, P):
                     nc.tensor.matmul(acc[:, h, c : c + P], a[:, i, c : c + P], ident[:], start=True, stop=False, is_transpose=True)
                     nc.tensor.matmul(acc[:, h, c : c + P], e[i][:, c : c + P], ident[:], start=False, stop=True, is_transpose=True)
-            nc.scalar.copy(turned[u][:], acc[:].rearrange("p i v -> p (i v)"))
+            nc.scalar.copy(b_turned[u][:], acc[:].rearrange("p i v -> p (i v)"))
 
         def turn_back(u):
             acc = bank([P, 2 * V])
             for c in range(0, 2 * V, P):
-                nc.tensor.transpose(acc[:, c : c + P], turned[u][:, c : c + P], ident[:])
+                nc.tensor.transpose(acc[:, c : c + P], b_turned[u][:, c : c + P], ident[:])
             nc.scalar.copy(b[u][:].rearrange("p i v -> p (i v)"), acc[:])
 
         def get_d(i):
             nc.vector.tensor_tensor(d[:, i, :], q[:, i, :], e[i][:], ALU.mult)
 
-        def negate(i, tag):
-            nd[i] = keep.tile([P, V], F32, name="nd%d" % i, tag=tag, align_bytes=64)
-            nc.scalar.activation(nd[i][:], d[:, i, :], ACT.Copy, scale=-1.0)
+        def negate_d(i):
+            minus_d[i] = sb("minus_d%d" % i, [P, V], F32)
+            nc.scalar.activation(minus_d[i][:], d[:, i, :], ACT.Copy, scale=-1.0)
 
-        def put_a(i, tag):
-            z[i] = keep.tile([P, S if i < 2 else 2 * S], F32, name="z%d" % i, tag=tag, align_bytes=64)
+        def put_na(i, reuses=None):
+            z[i] = sb("z%d" % i, [P, S if i < 2 else 2 * S], F32, reuses)
             nc.vector.tensor_tensor(z[i][:].indirect(la_t[:]), a[:, i, :], d[:, i, :], ALU.add)
 
-        def put_b(i):
-            nc.vector.tensor_tensor(z[i][:].indirect(lb_t[:]), b[i // 2][:, i % 2, :], nd[i][:], ALU.add)
+        def put_nb(i):
+            nc.vector.tensor_tensor(z[i][:].indirect(lb_t[:]), b[i // 2][:, i % 2, :], minus_d[i][:], ALU.add)
 
         def weave(i, copies):
             n = S // len(copies)
             pair = z[i][:].rearrange("p (r s) -> p s r", r=2)
             for c, copy in enumerate(copies):
-                copy(z_b[:, n * c : n * c + n, order[i] : order[i] + 2], pair[:, n * c : n * c + n, :])
+                copy(z_b[:, n * c : n * c + n, PLANE[i] : PLANE[i] + 2], pair[:, n * c : n * c + n, :])
 
         halves = (slice(0, S // 2), slice(S // 2, S))
+        chunks = [slice(c, c + CHUNK) for c in range(0, S, CHUNK)]
         make_y(0, halves[0], nc.scalar.copy)
-        make_y(0, halves[1], nc.vector.tensor_copy)
-        make_y(1, halves[0], nc.scalar.copy)
-        make_y(1, halves[1], nc.scalar.copy)
-        make_y(2, slice(0, S), nc.scalar.copy)
-        make_y(3, slice(0, S), nc.scalar.copy)
+        make_y(0, chunks[2], nc.scalar.copy)
+        make_y(0, chunks[3], nc.vector.tensor_copy)
+        deal(w2_c, w2_raw, LINE_WORDS)
+        for i in range(1, PACK):
+            make_y(i, slice(0, S), nc.scalar.copy)
         for i in range(PACK):
             multiply_gate(i)
-        get_a(0, 2)
-        get_e(0, "e0", 2)
+
+        get_a(0, pieces=2)
+        get_e(0, pieces=2)
         get_a(1)
         get_a(2)
-        get_e(1, "w1_s")
+        get_e(1, reuses="w2_c")
         get_a(3)
-        get_e(2, "w2_s")
-        for step in (make_pre, make_q):
+        get_e(2, reuses="w2_s")
+        for step in (copy_gate, get_q):
             step(0)
             step(1)
         get_d(0)
         get_d(1)
-        get_e(3, "pre1")
-        put_a(0, "z0")
-        for step in (make_pre, make_q):
+        get_e(3, reuses="pre1")
+        put_na(0)
+        for step in (copy_gate, get_q):
             step(2)
             step(3)
         get_d(2)
         get_d(3)
-        put_a(1, "pre3")
-        put_a(2, "pre2")
-        put_a(3, "z3")
+
+        put_na(1, reuses="pre3")
+        put_na(2, reuses="pre2")
+        put_na(3)
         add_turned(0)
         add_turned(1)
-        for i in range(3):
-            negate(i, "nd%d" % i)
+        for i in range(PACK - 1):
+            negate_d(i)
         turn_back(0)
         turn_back(1)
-        negate(3, "nd3")
+        negate_d(PACK - 1)
         for i in range(2):
-            put_b(i)
+            put_nb(i)
             nc.scalar.copy(z[i + 2][:, S : 2 * S], z[i][:])
-        put_b(2)
+        put_nb(2)
         weave(2, [nc.scalar.copy] * 2)
-        w3_c = keep.tile([P, N], I32, name="w3_c", tag="z0", align_bytes=64)
-        deal(w3_c, w3_raw, 4)
+
+        w3_planes = w3_raw[:].rearrange("p (b i t) -> p b t i", t=PACK, i=LINE_WORDS)
+        w3_first = sb("w3_first", [P, P], I32, reuses="z0")
+        nc.vector.tensor_copy(w3_first[:].rearrange("p (b i) -> p b i", i=LINE_WORDS), w3_planes[:, :, 0, :])
         idle = bank([P, S])
-        for w in range(WARM):
-            mm(idle[:], w3_c[:], w3_s[:], w, gw[:], gs[:])
-        put_b(3)
+        for warm_pass in range(WARM_PASSES):
+            mm(idle[:], w3_first[:], w3_s[:, plane_cols(0)], gw[:], gs[:])
+        put_nb(3)
+        w3_rest = sb("w3_rest", [P, N - P], I32, reuses="pre3")
+        nc.vector.tensor_copy(w3_rest[:].rearrange("p (t b i) -> p b t i", t=PACK - 1, i=LINE_WORDS), w3_planes[:, :, 1:PACK, :])
+        w3_c = [w3_first[:]] + [w3_rest[:, plane_cols(t)] for t in range(PACK - 1)]
         weave(3, [nc.vector.tensor_copy] * 2 + [nc.scalar.copy] * 2)
 
         z_s = sb("z_s", [P, S], U8)
@@ -260,29 +283,26 @@ def tile_picked_swapgate_sigmoid_po_kernel(
         o_s = sb("o_s", [P, S], U8)
         out_rows = out_0.rearrange("(p t) s -> p t s", t=PACK)
         out_words = words_of(out_1)
-        chunks = [slice(c, c + CH) for c in range(0, S, CH)]
 
-        def quant(codes, scales, src):
-            nc.vector.quantize_mx(out=codes.bitcast(FP8X4), scales=scales, in_=src.rearrange("p s t -> p (s t)"))
-
-        o_tiles = [sb("o0", [P, PACK, CH], F32), sb("o1", [P, PACK, CH], F32), sb("o23", [P, PACK, 2 * CH], F32)]
-        o = [o_tiles[0][:], o_tiles[1][:], o_tiles[2][:, :, 0:CH], o_tiles[2][:, :, CH : 2 * CH]]
-        accs = {}
+        o_tiles = [sb("o0", [P, PACK, CHUNK], F32), sb("o1", [P, PACK, CHUNK], F32), sb("o23", [P, PACK, 2 * CHUNK], F32)]
+        o = [o_tiles[0][:], o_tiles[1][:], o_tiles[2][:, :, 0:CHUNK], o_tiles[2][:, :, CHUNK : 2 * CHUNK]]
         z_c = sb("z_c", [P, S], U32)
         for cols in chunks:
             quant(z_c[:, cols], z_s[:, cols], z_b[:, cols, :])
+        out_banks = []
         for c, cols in enumerate(chunks):
-            accs[c] = bank([P, PACK, CH])
+            out_banks.append(bank([P, PACK, CHUNK]))
             for t in range(PACK):
-                mm(accs[c][:, t, :], w3_c[:], w3_s[:], t, z_c[:, cols], z_s[:, cols])
+                mm(out_banks[c][:, t, :], w3_c[t], w3_s[:, plane_cols(t)], z_c[:, cols], z_s[:, cols])
             copy = nc.vector.tensor_copy if c == 1 else nc.scalar.copy
-            copy(o[c], accs[c][:])
+            copy(o[c], out_banks[c][:])
             if c < 2:
                 nc.sync.dma_start(out_rows[:, :, cols], o[c])
-        nc.sync.dma_start(out_rows[:, :, 2 * CH : S], o_tiles[2][:])
+        nc.sync.dma_start(out_rows[:, :, halves[1]], o_tiles[2][:])
+
         for c in range(3):
             nc.vector.tensor_copy(o_b[:, chunks[c], :], o[c].rearrange("p t s -> p s t"))
-        nc.scalar.copy(o_b[:, chunks[3], :], accs[3][:].rearrange("p t s -> p s t"))
+        nc.scalar.copy(o_b[:, chunks[3], :], out_banks[3][:].rearrange("p t s -> p s t"))
         for cols in (halves[0], chunks[2], chunks[3]):
             quant(o_c[:, cols], o_s[:, cols], o_b[:, cols, :])
         for cols in halves:

@@ -263,7 +263,7 @@ def tile_picked_swapgate_sigmoid_po_kernel(
             put_nb(i)
             nc.scalar.copy(z[i + 2][:, S : 2 * S], z[i][:])
         put_nb(2)
-        weave(2, [nc.scalar.copy] * 2)
+        weave(2, [nc.scalar.copy])
 
         w3_planes = w3_raw[:].rearrange("p (b i t) -> p b t i", t=PACK, i=LINE_WORDS)
         w3_first = sb("w3_first", [P, P], I32, reuses="z0")
@@ -284,29 +284,31 @@ def tile_picked_swapgate_sigmoid_po_kernel(
         out_rows = out_0.rearrange("(p t) s -> p t s", t=PACK)
         out_words = words_of(out_1)
 
-        o_tiles = [sb("o0", [P, PACK, CHUNK], F32), sb("o1", [P, PACK, CHUNK], F32), sb("o23", [P, PACK, 2 * CHUNK], F32)]
-        o = [o_tiles[0][:], o_tiles[1][:], o_tiles[2][:, :, 0:CHUNK], o_tiles[2][:, :, CHUNK : 2 * CHUNK]]
+        o = [sb("o%d" % c, [P, PACK, CHUNK], F32)[:] for c in range(len(chunks))]
         z_c = sb("z_c", [P, S], U32)
         for cols in chunks:
             quant(z_c[:, cols], z_s[:, cols], z_b[:, cols, :])
-        out_banks = []
-        for c, cols in enumerate(chunks):
-            out_banks.append(bank([P, PACK, CHUNK]))
-            for t in range(PACK):
-                mm(out_banks[c][:, t, :], w3_c[t], w3_s[:, plane_cols(t)], z_c[:, cols], z_s[:, cols])
-            copy = nc.vector.tensor_copy if c == 1 else nc.scalar.copy
-            copy(o[c], out_banks[c][:])
-            if c < 2:
-                nc.sync.dma_start(out_rows[:, :, cols], o[c])
-        nc.sync.dma_start(out_rows[:, :, halves[1]], o_tiles[2][:])
+        def multiply_out(c, planes):
+            acc = bank([P, len(planes), CHUNK])
+            for j, t in enumerate(planes):
+                mm(acc[:, j, :], w3_c[t], w3_s[:, plane_cols(t)], z_c[:, chunks[c]], z_s[:, chunks[c]])
+            return acc
+
+        for c in range(3):
+            for first in (0, 2):
+                copy = nc.vector.tensor_copy if c < 2 and first else nc.scalar.copy
+                copy(o[c][:, first : first + 2, :], multiply_out(c, (first, first + 1))[:])
+            nc.sync.dma_start(out_rows[:, :, chunks[c]], o[c])
+        last_bank = multiply_out(3, range(PACK))
+        nc.scalar.copy(o[3], last_bank[:])
+        nc.sync.dma_start(out_rows[:, :, chunks[3]], o[3])
 
         for c in range(3):
             nc.vector.tensor_copy(o_b[:, chunks[c], :], o[c].rearrange("p t s -> p s t"))
-        nc.scalar.copy(o_b[:, chunks[3], :], out_banks[3][:].rearrange("p t s -> p s t"))
+        nc.scalar.copy(o_b[:, chunks[3], :], last_bank[:].rearrange("p t s -> p s t"))
         for cols in (halves[0], chunks[2], chunks[3]):
             quant(o_c[:, cols], o_s[:, cols], o_b[:, cols, :])
-        for cols in halves:
-            nc.sync.dma_start(out_words[:, cols], o_c[:, cols].bitcast(I32))
+        nc.sync.dma_start(out_words, o_c[:].bitcast(I32))
         for g in range(4):
             queue = nc.scalar if g % 2 else nc.sync
             queue.dma_start(out_2[0, 4 * g : 4 * g + 4, :].bitcast(I32), o_s[32 * g : 32 * g + 4, :].bitcast(I32))

@@ -23,12 +23,14 @@ LIST = 16
 BLOCKS = 16
 UPPER = P - BLOCKS
 LOWER = P - 2 * BLOCKS
+ROW_BYTES = 4 * S
 LINE_WORDS = 4
 LINE_BYTES = 16
 VECTOR_SHARE = 80
 WARM_PASSES = 3
 
 PLANE = (1, 3, 0, 2)
+ARRIVAL = (0, 3, 1, 2)
 
 
 def words_of(packed):
@@ -41,6 +43,7 @@ def tile_picked_swapgate_sigmoid_po_kernel(
     nc = tc.nc
     with ExitStack() as ctx:
         keep = ctx.enter_context(tc.tile_pool(name="keep", bufs=1))
+        placed = ctx.enter_context(tc.tile_pool(name="placed", bufs=1))
         psum = ctx.enter_context(tc.psum_pool(name="psum", bufs=8))
 
         def sb(name, shape, dtype, reuses=None):
@@ -121,10 +124,11 @@ def tile_picked_swapgate_sigmoid_po_kernel(
             copy(w1_b[:, :, ms, 0:2].rearrange("p t m j -> p m t j"), w1_r[0][:, :, ms].rearrange("p t m j -> p m t j"))
         for copy, ms in ((nc.vector.tensor_copy, slice(0, P // 2)), (nc.scalar.copy, slice(P // 2, P))):
             copy(w1_b[:, PLANE[0], ms, 2:PACK], w1_r[1][:, PLANE[0], ms])
-        nc.vector.tensor_copy(w1_b[:, PLANE[1], :, 2:PACK], w1_r[1][:, PLANE[1]])
-        for t in PLANE[2:]:
+        planes = [PLANE[i] for i in ARRIVAL]
+        nc.vector.tensor_copy(w1_b[:, planes[1], :, 2:PACK], w1_r[1][:, planes[1]])
+        for t in planes[2:]:
             nc.scalar.copy(w1_b[:, t, :, 2:PACK], w1_r[1][:, t])
-        for t in PLANE:
+        for t in planes:
             quant(w1_c[:, plane_cols(t)], w1_s[:, plane_cols(t)], w1_b[:, t])
 
         w2_c = sb("w2_c", [P, H], I32)
@@ -144,13 +148,14 @@ def tile_picked_swapgate_sigmoid_po_kernel(
         make_identity(nc, ident[:])
 
         y = [sb("y%d" % i, [P, S], F32) for i in range(PACK)]
-        pre = [sb("pre%d" % i, [P, S], F32) for i in range(PACK)]
+        pre = [sb("pre%d" % i, [P, S], F32) for i in range(PACK - 1)]
+        pre.append(placed.tile([P, S], F32, name="pre3", offset=ROW_BYTES // 2))
         q = sb("q", [P, PACK, V], F32)
         a = sb("a", [P, PACK, V], F32)
         e = {}
         b_turned = [sb("b_turned%d" % u, [P, 2 * V], F32) for u in range(2)]
         b = [sb("b%d" % u, [P, 2, V], F32) for u in range(2)]
-        d = sb("d", [P, PACK, V], F32)
+        d = {}
         minus_d = {}
         z = {}
         z_b = sb("z_b", [P, S, PACK], BF16)
@@ -176,8 +181,7 @@ def tile_picked_swapgate_sigmoid_po_kernel(
             for v in range(0, V, n):
                 nc.vector.tensor_copy(a[:, i, v : v + n], y[i][:].indirect(la_t[:, v // LIST : (v + n) // LIST]))
 
-        def get_e(i, reuses=None, pieces=1):
-            e[i] = sb("e%d" % i, [P, V], F32, reuses)
+        def get_e(i, pieces=1):
             n = V // pieces
             for v in range(0, V, n):
                 window = y[i][:].indirect(lb_t[:, v // LIST : (v + n) // LIST])
@@ -199,15 +203,20 @@ def tile_picked_swapgate_sigmoid_po_kernel(
             nc.scalar.copy(b[u][:].rearrange("p i v -> p (i v)"), acc[:])
 
         def get_d(i):
-            nc.vector.tensor_tensor(d[:, i, :], q[:, i, :], e[i][:], ALU.mult)
+            d[i] = sb("d%d" % i, [P, V], F32)[:]
+            nc.vector.tensor_tensor(d[i], q[:, i, :], e[i], ALU.mult)
 
         def negate_d(i):
             minus_d[i] = sb("minus_d%d" % i, [P, V], F32)
-            nc.scalar.activation(minus_d[i][:], d[:, i, :], ACT.Copy, scale=-1.0)
+            nc.scalar.activation(minus_d[i][:], d[i], ACT.Copy, scale=-1.0)
 
-        def put_na(i, reuses=None):
-            z[i] = sb("z%d" % i, [P, S if i < 2 else 2 * S], F32, reuses)
-            nc.vector.tensor_tensor(z[i][:].indirect(la_t[:]), a[:, i, :], d[:, i, :], ALU.add)
+        def la_window(i):
+            shape = [P, S if i < 2 else 2 * S]
+            if i in (1, 2):
+                z[i] = placed.tile(shape, F32, name="z%d" % i, offset=ROW_BYTES * (i - 1))
+            else:
+                z[i] = sb("z%d" % i, shape, F32)
+            return z[i][:].indirect(la_t[:])
 
         def put_nb(i):
             nc.vector.tensor_tensor(z[i][:].indirect(lb_t[:]), b[i // 2][:, i % 2, :], minus_d[i][:], ALU.add)
@@ -224,34 +233,42 @@ def tile_picked_swapgate_sigmoid_po_kernel(
         make_y(0, chunks[2], nc.scalar.copy)
         make_y(0, chunks[3], nc.vector.tensor_copy)
         deal(w2_c, w2_raw, LINE_WORDS)
-        for i in range(1, PACK):
+        for i in ARRIVAL[1:]:
             make_y(i, slice(0, S), nc.scalar.copy)
         for i in range(PACK):
             multiply_gate(i)
 
+        e[0] = sb("e0", [P, V], F32)[:]
         get_a(0, pieces=2)
         get_e(0, pieces=2)
-        get_a(1)
-        get_a(2)
-        get_e(1, reuses="w2_c")
-        get_a(3)
-        get_e(2, reuses="w2_s")
-        for step in (copy_gate, get_q):
-            step(0)
-            step(1)
+        for i in ARRIVAL[1:]:
+            get_a(i)
+        e[3] = sb("e3", [P, V], F32, reuses="w2_c")[:]
+        get_e(3)
+        copy_gate(0)
+        copy_gate(1)
+        get_q(0)
+        copy_gate(2)
+        get_q(1)
+        get_q(2)
+        copy_gate(3)
+        get_q(3)
         get_d(0)
-        get_d(1)
-        get_e(3, reuses="pre1")
-        put_na(0)
-        for step in (copy_gate, get_q):
-            step(2)
-            step(3)
-        get_d(2)
+        e_mid = sb("e_mid", [P, 2, V], F32, reuses="pre0")
+        e[1], e[2] = e_mid[:, 0, :], e_mid[:, 1, :]
+        get_e(1)
+        na_first = sb("na_first", [P, V], F32)
+        nc.vector.tensor_tensor(na_first[:], a[:, 0, :], d[0], ALU.add)
+        get_e(2)
+
+        nc.vector.tensor_copy(la_window(0), na_first[:])
+        d_mid = sb("d_mid", [P, 2, V], F32, reuses="y2")
+        nc.gpsimd.tensor_tensor(d_mid[:], q[:, 1:3, :], e_mid[:], ALU.mult)
+        d[1], d[2] = d_mid[:, 0, :], d_mid[:, 1, :]
         get_d(3)
 
-        put_na(1, reuses="pre3")
-        put_na(2, reuses="pre2")
-        put_na(3)
+        for i in range(1, PACK):
+            nc.vector.tensor_tensor(la_window(i), a[:, i, :], d[i], ALU.add)
         add_turned(0)
         add_turned(1)
         for i in range(PACK - 1):
@@ -272,7 +289,7 @@ def tile_picked_swapgate_sigmoid_po_kernel(
         for warm_pass in range(WARM_PASSES):
             mm(idle[:], w3_first[:], w3_s[:, plane_cols(0)], gw[:], gs[:])
         put_nb(3)
-        w3_rest = sb("w3_rest", [P, N - P], I32, reuses="pre3")
+        w3_rest = placed.tile([P, N - P], I32, name="w3_rest", offset=0, align_bytes=64)
         nc.vector.tensor_copy(w3_rest[:].rearrange("p (t b i) -> p b t i", t=PACK - 1, i=LINE_WORDS), w3_planes[:, :, 1:PACK, :])
         w3_c = [w3_first[:]] + [w3_rest[:, plane_cols(t)] for t in range(PACK - 1)]
         weave(3, [nc.vector.tensor_copy] * 2 + [nc.scalar.copy] * 2)

@@ -1,7 +1,6 @@
 from contextlib import ExitStack
 
 import concourse.mybir as mybir
-from concourse.masks import make_identity
 
 K, T, S, V, N, H = 512, 2048, 512, 256, 512, 512
 FLOPS = 2 * K * H * S * 2 + 2 * H * N * S
@@ -24,13 +23,13 @@ BLOCKS = 16
 UPPER = P - BLOCKS
 LOWER = P - 2 * BLOCKS
 ROW_BYTES = 4 * S
+BASE = 2 * ROW_BYTES - 128
 LINE_WORDS = 4
 LINE_BYTES = 16
 VECTOR_SHARE = 80
 WARM_PASSES = 3
 
-PLANE = (1, 3, 0, 2)
-ARRIVAL = (0, 3, 1, 2)
+PLANE = (3, 1, 2, 0)
 
 
 def words_of(packed):
@@ -44,33 +43,38 @@ def tile_picked_swapgate_sigmoid_po_kernel(
     with ExitStack() as ctx:
         keep = ctx.enter_context(tc.tile_pool(name="keep", bufs=1))
         placed = ctx.enter_context(tc.tile_pool(name="placed", bufs=1))
-        psum = ctx.enter_context(tc.psum_pool(name="psum", bufs=8))
+        psum = ctx.enter_context(tc.psum_pool(name="psum", bufs=1))
 
         def sb(name, shape, dtype, reuses=None):
             return keep.tile(shape, dtype, name=name, tag=reuses or name, align_bytes=64)
 
-        def bank(shape):
-            return psum.tile(shape, F32, name="bank")
+        def at(name, shape, dtype, offset):
+            return placed.tile(shape, dtype, name=name, offset=offset, align_bytes=64)
+
+        def bank(number, shape):
+            return psum.tile(shape, F32, name="bank%d" % number)
 
         offs_t = keep.tile([P, S // LIST], U16, name="offs_t")
         la_t = keep.tile([P, V // LIST], U16, name="la_t")
         lb_t = keep.tile([P, V // LIST], U16, name="lb_t")
         xw = sb("xw", [P, T], U32)
-        xs = sb("xs", [P, T], U8)
+        xs = at("xs", [P, T], U8, 5 * ROW_BYTES)
         ws_raw = sb("ws_raw", [P, H], U8)
         w1_raw = [sb("w1_raw%d" % u, [P, 2, H], F32) for u in range(2)]
         gs = sb("gs", [P, S], U8)
-        w2_s = sb("w2_s", [P, H], U8)
-        w3_s = sb("w3_s", [P, N], U8)
 
         warm = sb("warm", [P, 2], F32)
-        nc.gpsimd.memset(xs[0:LOWER, :].bitcast(I32), 0)
-        nc.gpsimd.memset(xs[LOWER:UPPER, :].bitcast(I32), 0)
         nc.vector.memset(warm[:, 0:1], 0.0)
-        nc.vector.memset(ws_raw[0:LOWER, :].bitcast(I32), 0)
+        nc.vector.memset(xs[0:LOWER, :].bitcast(I32), 0)
+        nc.vector.memset(xs[LOWER:UPPER, :].bitcast(I32), 0)
         nc.vector.memset(gs[:].bitcast(I32), 0)
-        nc.vector.memset(w2_s[:].bitcast(I32), 0)
-        nc.vector.memset(w3_s[:].bitcast(I32), 0)
+        nc.gpsimd.memset(ws_raw[:].bitcast(I32), 0)
+
+        def load_scales(queue, raw, scales, groups):
+            for g in groups:
+                queue.dma_start(raw[32 * g : 32 * g + 4, :].bitcast(I32), scales[0, 4 * g : 4 * g + 4, :].bitcast(I32))
+
+        load_scales(nc.gpsimd, ws_raw, w2_scales, range(4))
         nc.scalar.activation(warm[:, 1:2], warm[:, 0:1], ACT.Sigmoid)
 
         def place_scales(dst, src, first):
@@ -79,19 +83,17 @@ def tile_picked_swapgate_sigmoid_po_kernel(
 
         w1_rows = w1.rearrange("(p j) c -> p j c", j=PACK)
         nc.sync.dma_start(offs_t[:], offs)
+        nc.sync.dma_start(la_t[:], la)
         nc.scalar.dma_start(xs[UPPER:P, :].bitcast(I32), x_scales[0].bitcast(I32))
         nc.sync.dma_start(xw[:].bitcast(I32), words_of(x_words))
-        nc.sync.dma_start(ws_raw[LOWER:UPPER, :].bitcast(I32), w2_scales[0].bitcast(I32))
-        nc.sync.dma_start(ws_raw[UPPER:P, :].bitcast(I32), w3_scales[0].bitcast(I32))
         for u in range(2):
             nc.sync.dma_start(w1_raw[u][:], w1_rows[:, 2 * u : 2 * u + 2, :])
-        nc.sync.dma_start(la_t[:], la)
         nc.sync.dma_start(lb_t[:], lb)
 
         gs_raw = sb("gs_raw", [P, S], U8)
         nc.vector.tensor_copy(gs_raw[:], xs[:].indirect(offs_t[:]))
         place_scales(gs, gs_raw, UPPER)
-        w2_raw = sb("w2_raw", [P, H], I32, reuses="xs")
+        w2_raw = at("w2_raw", [P, H], I32, 5 * ROW_BYTES)
         nc.sync.dma_start(w2_raw[:], words_of(w2_words))
 
         gw = sb("gw", [P, S], U32)
@@ -102,17 +104,9 @@ def tile_picked_swapgate_sigmoid_po_kernel(
                 dst[:].rearrange("p (t b i) -> p b t i", t=PACK, i=run), src[:].rearrange("p (b i t) -> p b t i", t=PACK, i=run)
             )
 
-        ws_dealt = sb("ws_dealt", [P, H], U8)
-        deal(ws_dealt, ws_raw, LINE_BYTES)
-        place_scales(w2_s, ws_dealt, LOWER)
-        w3_raw = sb("w3_raw", [P, N], I32, reuses="ws_raw")
-        nc.sync.dma_start(w3_raw[:], words_of(w3_words))
-        place_scales(w3_s, ws_dealt, UPPER)
 
         w1_b = sb("w1_b", [P, PACK, P, PACK], BF16)
         w1_r = [w1_raw[u][:].rearrange("p j (m t) -> p t m j", t=PACK) for u in range(2)]
-        w1_c = sb("w1_c", [P, H], U32)
-        w1_s = sb("w1_s", [P, H], U8)
 
         def quant(codes, scales, src):
             nc.vector.quantize_mx(out=codes.bitcast(FP8X4), scales=scales, in_=src.rearrange("p s t -> p (s t)"))
@@ -122,16 +116,21 @@ def tile_picked_swapgate_sigmoid_po_kernel(
 
         for copy, ms in ((nc.vector.tensor_copy, slice(0, VECTOR_SHARE)), (nc.scalar.copy, slice(VECTOR_SHARE, P))):
             copy(w1_b[:, :, ms, 0:2].rearrange("p t m j -> p m t j"), w1_r[0][:, :, ms].rearrange("p t m j -> p m t j"))
+
+        def round_rest(i, copy):
+            copy(w1_b[:, PLANE[i], :, 2:PACK], w1_r[1][:, PLANE[i]])
+
         for copy, ms in ((nc.vector.tensor_copy, slice(0, P // 2)), (nc.scalar.copy, slice(P // 2, P))):
             copy(w1_b[:, PLANE[0], ms, 2:PACK], w1_r[1][:, PLANE[0], ms])
-        planes = [PLANE[i] for i in ARRIVAL]
-        nc.vector.tensor_copy(w1_b[:, planes[1], :, 2:PACK], w1_r[1][:, planes[1]])
-        for t in planes[2:]:
-            nc.scalar.copy(w1_b[:, t, :, 2:PACK], w1_r[1][:, t])
-        for t in planes:
-            quant(w1_c[:, plane_cols(t)], w1_s[:, plane_cols(t)], w1_b[:, t])
+        round_rest(1, nc.vector.tensor_copy)
+        for i in (2, 3):
+            round_rest(i, nc.scalar.copy)
 
-        w2_c = sb("w2_c", [P, H], I32)
+        w3_raw = sb("w3_raw", [P, N], I32, reuses="w1_raw0")
+        nc.sync.dma_start(w3_raw[:], words_of(w3_words))
+        w3_s_raw = sb("w3_s_raw", [P, N], U8, reuses="xw")
+        nc.gpsimd.memset(w3_s_raw[:].bitcast(I32), 0)
+        load_scales(nc.sync, w3_s_raw, w3_scales, range(4))
 
         def mm(dst, weights, weight_scales, moving, moving_scales):
             nc.tensor.matmul_mx(
@@ -144,82 +143,70 @@ def tile_picked_swapgate_sigmoid_po_kernel(
                 stop=True,
             )
 
-        ident = sb("ident", [P, P], F32)
-        make_identity(nc, ident[:])
+        w1_c, w1_s, y, pre, y_banks, gate_banks = {}, {}, {}, {}, {}, {}
+        a, b, q, e, d, minus_d, z = {}, {}, {}, {}, {}, {}, {}
+        w2_c = {}
 
-        y = [sb("y%d" % i, [P, S], F32) for i in range(PACK)]
-        pre = [sb("pre%d" % i, [P, S], F32) for i in range(PACK - 1)]
-        pre.append(placed.tile([P, S], F32, name="pre3", offset=ROW_BYTES // 2))
-        q = sb("q", [P, PACK, V], F32)
-        a = sb("a", [P, PACK, V], F32)
-        e = {}
-        b_turned = [sb("b_turned%d" % u, [P, 2 * V], F32) for u in range(2)]
-        b = [sb("b%d" % u, [P, 2, V], F32) for u in range(2)]
-        d = {}
-        minus_d = {}
-        z = {}
-        z_b = sb("z_b", [P, S, PACK], BF16)
-        gate_banks = {}
+        def deal_planes(into, name, raw, dtype, run, planes, reuses=None):
+            dealt = sb(name, [P, len(planes), P], dtype, reuses)
+            for j, t in enumerate(planes):
+                into[t] = dealt[:, j, :]
+            source = raw[:].rearrange("p (b i t) -> p b t i", t=PACK, i=run)
+            nc.vector.tensor_copy(dealt[:].rearrange("p t (b i) -> p b t i", i=run), source[:, :, planes.start : planes.stop, :])
 
-        def make_y(i, cols, copy):
-            acc = bank([P, cols.stop - cols.start])
-            mm(acc[:], w1_c[:, plane_cols(PLANE[i])], w1_s[:, plane_cols(PLANE[i])], gw[:, cols], gs[:, cols])
-            copy(y[i][:, cols], acc[:])
+        halves = (slice(0, S // 2), slice(S // 2, S))
+        chunks = [slice(c, c + CHUNK) for c in range(0, S, CHUNK)]
+        whole = slice(0, S)
 
-        def multiply_gate(i):
-            gate_banks[i] = bank([P, S])
-            mm(gate_banks[i][:], w2_c[:, plane_cols(PLANE[i])], w2_s[:, plane_cols(PLANE[i])], gw[:], gs[:])
+        def quant_w1(i, codes):
+            w1_c[i] = codes
+            w1_s[i] = sb("w1_s%d" % i, [P, P], U8)
+            quant(w1_c[i][:], w1_s[i][:], w1_b[:, PLANE[i]])
 
-        def copy_gate(i):
-            nc.scalar.copy(pre[i][:], gate_banks[i][:])
+        def multiply_y(i, cols, number):
+            acc = bank(number, [P, cols.stop - cols.start])
+            mm(acc[:], w1_c[i][:], w1_s[i][:], gw[:, cols], gs[:, cols])
+            return acc
 
-        def get_q(i):
-            nc.scalar.activation(q[:, i, :], pre[i][:].indirect(la_t[:]), ACT.Sigmoid)
+        def multiply_gate(i, cols, number):
+            acc = bank(number, [P, cols.stop - cols.start])
+            mm(acc[:], w2_c[PLANE[i]], ws_dealt[:, plane_cols(PLANE[i])], gw[:, cols], gs[:, cols])
+            return acc
 
-        def get_a(i, pieces=1):
-            n = V // pieces
-            for v in range(0, V, n):
-                nc.vector.tensor_copy(a[:, i, v : v + n], y[i][:].indirect(la_t[:, v // LIST : (v + n) // LIST]))
+        def empty(dst, acc):
+            for cols in halves:
+                nc.scalar.copy(dst[:, cols], acc[:, cols])
 
-        def get_e(i, pieces=1):
-            n = V // pieces
-            for v in range(0, V, n):
-                window = y[i][:].indirect(lb_t[:, v // LIST : (v + n) // LIST])
-                nc.vector.tensor_tensor(e[i][:, v : v + n], window, a[:, i, v : v + n], ALU.subtract)
+        def short(name, i, reuses=None):
+            return sb("%s%d" % (name, i), [P, V], F32, reuses)
 
-        def add_turned(u):
-            acc = bank([P, 2, V])
-            for h in range(2):
-                i = 2 * u + h
-                for c in range(0, V, P):
-                    nc.tensor.matmul(acc[:, h, c : c + P], a[:, i, c : c + P], ident[:], start=True, stop=False, is_transpose=True)
-                    nc.tensor.matmul(acc[:, h, c : c + P], e[i][:, c : c + P], ident[:], start=False, stop=True, is_transpose=True)
-            nc.scalar.copy(b_turned[u][:], acc[:].rearrange("p i v -> p (i v)"))
+        def get_ab(i, reuses=None):
+            both = sb("ab%d" % i, [P, 2, V], F32, reuses)
+            a[i], b[i] = both[:, 0, :], both[:, 1, :]
+            nc.scalar.activation(a[i], y[i][:].indirect(la_t[:]), ACT.Copy)
+            nc.scalar.activation(b[i], y[i][:].indirect(lb_t[:]), ACT.Copy)
 
-        def turn_back(u):
-            acc = bank([P, 2 * V])
-            for c in range(0, 2 * V, P):
-                nc.tensor.transpose(acc[:, c : c + P], b_turned[u][:, c : c + P], ident[:])
-            nc.scalar.copy(b[u][:].rearrange("p i v -> p (i v)"), acc[:])
+        def get_q(i, tile=None):
+            q[i] = short("q", i) if tile is None else tile
+            nc.scalar.activation(q[i][:], pre[i][:].indirect(la_t[:]), ACT.Sigmoid)
+
+        def get_e(i, reuses=None):
+            e[i] = short("e", i, reuses)
+            nc.vector.tensor_tensor(e[i][:], b[i][:], a[i][:], ALU.subtract)
 
         def get_d(i):
-            d[i] = sb("d%d" % i, [P, V], F32)[:]
-            nc.vector.tensor_tensor(d[i], q[:, i, :], e[i], ALU.mult)
+            d[i] = short("d", i)
+            nc.vector.tensor_tensor(d[i][:], q[i][:], e[i][:], ALU.mult)
 
-        def negate_d(i):
-            minus_d[i] = sb("minus_d%d" % i, [P, V], F32)
-            nc.scalar.activation(minus_d[i][:], d[i], ACT.Copy, scale=-1.0)
+        def negate_d(i, offset=None):
+            minus_d[i] = short("minus_d", i) if offset is None else at("minus_d%d" % i, [P, V], F32, offset)
+            nc.scalar.activation(minus_d[i][:], d[i][:], ACT.Copy, scale=-1.0)
 
-        def la_window(i):
-            shape = [P, S if i < 2 else 2 * S]
-            if i in (1, 2):
-                z[i] = placed.tile(shape, F32, name="z%d" % i, offset=ROW_BYTES * (i - 1))
-            else:
-                z[i] = sb("z%d" % i, shape, F32)
-            return z[i][:].indirect(la_t[:])
+        def put_na(i):
+            nc.vector.tensor_tensor(z[i][:].indirect(la_t[:]), a[i][:], d[i][:], ALU.add)
 
         def put_nb(i):
-            nc.vector.tensor_tensor(z[i][:].indirect(lb_t[:]), b[i // 2][:, i % 2, :], minus_d[i][:], ALU.add)
+            nc.vector.tensor_tensor(z[i][:].indirect(lb_t[:]), b[i][:], minus_d[i][:], ALU.add)
 
         def weave(i, copies):
             n = S // len(copies)
@@ -227,71 +214,111 @@ def tile_picked_swapgate_sigmoid_po_kernel(
             for c, copy in enumerate(copies):
                 copy(z_b[:, n * c : n * c + n, PLANE[i] : PLANE[i] + 2], pair[:, n * c : n * c + n, :])
 
-        halves = (slice(0, S // 2), slice(S // 2, S))
-        chunks = [slice(c, c + CHUNK) for c in range(0, S, CHUNK)]
-        make_y(0, halves[0], nc.scalar.copy)
-        make_y(0, chunks[2], nc.scalar.copy)
-        make_y(0, chunks[3], nc.vector.tensor_copy)
-        deal(w2_c, w2_raw, LINE_WORDS)
-        for i in ARRIVAL[1:]:
-            make_y(i, slice(0, S), nc.scalar.copy)
-        for i in range(PACK):
-            multiply_gate(i)
-
-        e[0] = sb("e0", [P, V], F32)[:]
-        get_a(0, pieces=2)
-        get_e(0, pieces=2)
-        for i in ARRIVAL[1:]:
-            get_a(i)
-        e[3] = sb("e3", [P, V], F32, reuses="w2_c")[:]
-        get_e(3)
-        copy_gate(0)
-        copy_gate(1)
+        quant_w1(0, sb("w1_c0", [P, P], U32))
+        ws_dealt = sb("ws_dealt", [P, H], U8, reuses="gs_raw")
+        deal(ws_dealt, ws_raw, LINE_BYTES)
+        deal_planes(w2_c, "w2_first", w2_raw, I32, LINE_WORDS, range(3, 4))
+        deal_planes(w2_c, "w2_rest", w2_raw, I32, LINE_WORDS, range(3))
+        quant_w1(1, at("w1_c1", [P, P], U32, 5 * ROW_BYTES))
+        y[0] = sb("y0", [P, S], F32)
+        for number, (copy, cols) in enumerate(zip((nc.scalar.copy, nc.scalar.copy, nc.scalar.copy), (halves[0], chunks[2], chunks[3]))):
+            copy(y[0][:, cols], multiply_y(0, cols, number)[:])
+        pre[0] = at("pre0", [P, S], F32, BASE + 64 - ROW_BYTES)
+        for cols, number in zip(halves, (3, 4)):
+            nc.scalar.copy(pre[0][:, cols], multiply_gate(0, cols, number)[:])
+        a[0] = at("a0", [P, V], F32, 5 * ROW_BYTES + 512)
+        e[0] = short("e", 0)
+        for v in (0, V // 2):
+            nc.vector.tensor_copy(a[0][:, v : v + V // 2], y[0][:].indirect(la_t[:, v // LIST : (v + V // 2) // LIST]))
+        for v in (0, V // 2):
+            window = y[0][:].indirect(lb_t[:, v // LIST : (v + V // 2) // LIST])
+            nc.vector.tensor_tensor(e[0][:, v : v + V // 2], window, a[0][:, v : v + V // 2], ALU.subtract)
+        y1_banks = [multiply_y(1, cols, number) for cols, number in zip(halves, (5, 4))]
+        gate_banks[1] = multiply_gate(1, whole, 6)
+        quant_w1(2, sb("w1_c2", [P, P], U32, reuses="w2_first"))
+        y_banks[2] = [multiply_y(2, cols, number) for cols, number in zip(halves, (7, 5))]
         get_q(0)
-        copy_gate(2)
-        get_q(1)
-        get_q(2)
-        copy_gate(3)
-        get_q(3)
         get_d(0)
-        e_mid = sb("e_mid", [P, 2, V], F32, reuses="pre0")
-        e[1], e[2] = e_mid[:, 0, :], e_mid[:, 1, :]
-        get_e(1)
-        na_first = sb("na_first", [P, V], F32)
-        nc.vector.tensor_tensor(na_first[:], a[:, 0, :], d[0], ALU.add)
-        get_e(2)
+        quant_w1(3, at("w1_c3", [P, P], U32, BASE + 64 - ROW_BYTES))
+        gate_banks[2] = multiply_gate(2, whole, 0)
+        y_banks[3] = [multiply_y(3, cols, number) for cols, number in zip(halves, (1, 3))]
+        gate_banks[3] = multiply_gate(3, whole, 2)
+        na, nb = {}, {}
 
-        nc.vector.tensor_copy(la_window(0), na_first[:])
-        d_mid = sb("d_mid", [P, 2, V], F32, reuses="y2")
-        nc.gpsimd.tensor_tensor(d_mid[:], q[:, 1:3, :], e_mid[:], ALU.mult)
-        d[1], d[2] = d_mid[:, 0, :], d_mid[:, 1, :]
-        get_d(3)
+        def two(engine, name, i, left, right, op, reuses=None):
+            out = short(name, i, reuses)
+            engine.tensor_tensor(out[:], left[:], right[:], op)
+            return out
 
-        for i in range(1, PACK):
-            nc.vector.tensor_tensor(la_window(i), a[:, i, :], d[i], ALU.add)
-        add_turned(0)
-        add_turned(1)
-        for i in range(PACK - 1):
-            negate_d(i)
-        turn_back(0)
-        turn_back(1)
-        negate_d(PACK - 1)
-        for i in range(2):
-            put_nb(i)
-            nc.scalar.copy(z[i + 2][:, S : 2 * S], z[i][:])
-        put_nb(2)
+        def put(i, offsets, values):
+            nc.vector.tensor_copy(z[i][:].indirect(offsets[:]), values[:])
+
+        def on_gpsimd(i, sums=True, reuses=None):
+            e[i] = two(nc.gpsimd, "e", i, b[i], a[i], ALU.subtract, reuses)
+            get_q(i, q_tiles[i]())
+            d[i] = two(nc.gpsimd, "d", i, q[i], e[i], ALU.mult)
+            if sums:
+                na[i] = two(nc.gpsimd, "na", i, a[i], d[i], ALU.add)
+                nb[i] = two(nc.gpsimd, "nb", i, b[i], d[i], ALU.subtract)
+
+        q_tiles = {
+            1: lambda: at("q1", [P, V], F32, BASE + 1088),
+            2: lambda: short("q", 2),
+            3: lambda: short("q", 3),
+        }
+        na[0] = two(nc.vector, "na", 0, a[0], d[0], ALU.add)
+        rest = two(nc.vector, "rest", 0, e[0], d[0], ALU.subtract)
+        z[0] = sb("z0", [P, S], F32)
+        put(0, la_t, na[0])
+        nb[0] = two(nc.gpsimd, "nb", 0, a[0], rest, ALU.add)
+
+        y[1] = at("y1", [P, S], F32, BASE + 64)
+        for cols, acc in zip(halves, y1_banks):
+            nc.scalar.copy(y[1][:, cols], acc[:])
+        get_ab(1)
+        pre[1] = sb("pre1", [P, S], F32)
+        empty(pre[1], gate_banks[1])
+        y[2] = sb("y2", [P, S], F32, reuses="rest0")
+        nc.vector.tensor_copy(y[2][:, halves[0]], y_banks[2][0][:])
+        put(0, lb_t, nb[0])
+        z[2] = sb("z2", [P, 2 * S], F32)
+        nc.sync.dma_start(z[2][:, S : 2 * S], z[0][:])
+        on_gpsimd(1, reuses="e0")
+        z[1] = sb("z1", [P, S], F32)
+        put(1, la_t, na[1])
+
+        nc.scalar.copy(y[2][:, halves[1]], y_banks[2][1][:])
+        get_ab(2, reuses="pre1")
+        pre[2] = sb("pre2", [P, S], F32)
+        empty(pre[2], gate_banks[2])
+        y[3] = sb("y3", [P, S], F32, reuses="d1")
+        nc.vector.tensor_copy(y[3][:, halves[0]], y_banks[3][0][:])
+        put(1, lb_t, nb[1])
+        on_gpsimd(2, reuses="ab1")
+        put(2, la_t, na[2])
+        put(2, lb_t, nb[2])
+
+        pre[3] = sb("pre3", [P, S], F32)
+        empty(pre[3], gate_banks[3])
+        nc.scalar.copy(y[3][:, halves[1]], y_banks[3][1][:])
+        get_ab(3, reuses="pre2")
+        on_gpsimd(3, sums=False, reuses="pre1")
+        z[3] = sb("z3", [P, 2 * S], F32, reuses="pre3")
+        nc.scalar.copy(z[3][:, S : 2 * S], z[1][:])
+        put_na(3)
+        negate_d(3)
+        z_b = sb("z_b", [P, S, PACK], BF16, reuses="q3")
         weave(2, [nc.scalar.copy])
 
-        w3_planes = w3_raw[:].rearrange("p (b i t) -> p b t i", t=PACK, i=LINE_WORDS)
-        w3_first = sb("w3_first", [P, P], I32, reuses="z0")
-        nc.vector.tensor_copy(w3_first[:].rearrange("p (b i) -> p b i", i=LINE_WORDS), w3_planes[:, :, 0, :])
-        idle = bank([P, S])
+        w3_dealt = sb("w3_dealt", [P, N], I32, reuses="pre1")
+        deal(w3_dealt, w3_raw, LINE_WORDS)
+        w3_c = [w3_dealt[:, plane_cols(t)] for t in range(PACK)]
+        idle = bank(3, [P, S])
         for warm_pass in range(WARM_PASSES):
-            mm(idle[:], w3_first[:], w3_s[:, plane_cols(0)], gw[:], gs[:])
+            mm(idle[:], w3_c[0], ws_dealt[:, plane_cols(0)], gw[:], gs[:])
         put_nb(3)
-        w3_rest = placed.tile([P, N - P], I32, name="w3_rest", offset=0, align_bytes=64)
-        nc.vector.tensor_copy(w3_rest[:].rearrange("p (t b i) -> p b t i", t=PACK - 1, i=LINE_WORDS), w3_planes[:, :, 1:PACK, :])
-        w3_c = [w3_first[:]] + [w3_rest[:, plane_cols(t)] for t in range(PACK - 1)]
+        w3_s = sb("w3_s", [P, N], U8, reuses="d3")
+        deal(w3_s, w3_s_raw, LINE_BYTES)
         weave(3, [nc.vector.tensor_copy] * 2 + [nc.scalar.copy] * 2)
 
         z_s = sb("z_s", [P, S], U8)
@@ -306,7 +333,7 @@ def tile_picked_swapgate_sigmoid_po_kernel(
         for cols in chunks:
             quant(z_c[:, cols], z_s[:, cols], z_b[:, cols, :])
         def multiply_out(c, planes):
-            acc = bank([P, len(planes), CHUNK])
+            acc = bank((4 + 2 * c + planes[0] // 2) % 8, [P, len(planes), CHUNK])
             for j, t in enumerate(planes):
                 mm(acc[:, j, :], w3_c[t], w3_s[:, plane_cols(t)], z_c[:, chunks[c]], z_s[:, chunks[c]])
             return acc

@@ -29,7 +29,7 @@ LINE_BYTES = 16
 VECTOR_SHARE = 80
 WARM_PASSES = 3
 
-PLANE = (3, 1, 2, 0)
+PLANE = (1, 3, 0, 2)
 
 
 def words_of(packed):
@@ -58,23 +58,21 @@ def tile_picked_swapgate_sigmoid_po_kernel(
         la_t = keep.tile([P, V // LIST], U16, name="la_t")
         lb_t = keep.tile([P, V // LIST], U16, name="lb_t")
         xw = sb("xw", [P, T], U32)
-        xs = at("xs", [P, T], U8, 5 * ROW_BYTES)
+        xs = sb("xs", [P, T], U8)
         ws_raw = sb("ws_raw", [P, H], U8)
         w1_raw = [sb("w1_raw%d" % u, [P, 2, H], F32) for u in range(2)]
         gs = sb("gs", [P, S], U8)
+        w2_s = sb("w2_s", [P, H], U8)
+        w3_s = sb("w3_s", [P, N], U8)
 
         warm = sb("warm", [P, 2], F32)
+        nc.gpsimd.memset(xs[0:LOWER, :].bitcast(I32), 0)
+        nc.gpsimd.memset(xs[LOWER:UPPER, :].bitcast(I32), 0)
         nc.vector.memset(warm[:, 0:1], 0.0)
-        nc.vector.memset(xs[0:LOWER, :].bitcast(I32), 0)
-        nc.vector.memset(xs[LOWER:UPPER, :].bitcast(I32), 0)
+        nc.vector.memset(ws_raw[0:LOWER, :].bitcast(I32), 0)
         nc.vector.memset(gs[:].bitcast(I32), 0)
-        nc.gpsimd.memset(ws_raw[:].bitcast(I32), 0)
-
-        def load_scales(queue, raw, scales, groups):
-            for g in groups:
-                queue.dma_start(raw[32 * g : 32 * g + 4, :].bitcast(I32), scales[0, 4 * g : 4 * g + 4, :].bitcast(I32))
-
-        load_scales(nc.gpsimd, ws_raw, w2_scales, range(4))
+        nc.vector.memset(w2_s[:].bitcast(I32), 0)
+        nc.vector.memset(w3_s[:].bitcast(I32), 0)
         nc.scalar.activation(warm[:, 1:2], warm[:, 0:1], ACT.Sigmoid)
 
         def place_scales(dst, src, first):
@@ -83,17 +81,19 @@ def tile_picked_swapgate_sigmoid_po_kernel(
 
         w1_rows = w1.rearrange("(p j) c -> p j c", j=PACK)
         nc.sync.dma_start(offs_t[:], offs)
-        nc.sync.dma_start(la_t[:], la)
         nc.scalar.dma_start(xs[UPPER:P, :].bitcast(I32), x_scales[0].bitcast(I32))
         nc.sync.dma_start(xw[:].bitcast(I32), words_of(x_words))
+        nc.sync.dma_start(ws_raw[LOWER:UPPER, :].bitcast(I32), w2_scales[0].bitcast(I32))
+        nc.sync.dma_start(ws_raw[UPPER:P, :].bitcast(I32), w3_scales[0].bitcast(I32))
         for u in range(2):
             nc.sync.dma_start(w1_raw[u][:], w1_rows[:, 2 * u : 2 * u + 2, :])
+        nc.sync.dma_start(la_t[:], la)
         nc.sync.dma_start(lb_t[:], lb)
 
         gs_raw = sb("gs_raw", [P, S], U8)
         nc.vector.tensor_copy(gs_raw[:], xs[:].indirect(offs_t[:]))
         place_scales(gs, gs_raw, UPPER)
-        w2_raw = at("w2_raw", [P, H], I32, 5 * ROW_BYTES)
+        w2_raw = sb("w2_raw", [P, H], I32, reuses="xs")
         nc.sync.dma_start(w2_raw[:], words_of(w2_words))
 
         gw = sb("gw", [P, S], U32)
@@ -104,9 +104,17 @@ def tile_picked_swapgate_sigmoid_po_kernel(
                 dst[:].rearrange("p (t b i) -> p b t i", t=PACK, i=run), src[:].rearrange("p (b i t) -> p b t i", t=PACK, i=run)
             )
 
+        ws_dealt = sb("ws_dealt", [P, H], U8)
+        deal(ws_dealt, ws_raw, LINE_BYTES)
+        place_scales(w2_s, ws_dealt, LOWER)
+        w3_raw = sb("w3_raw", [P, N], I32, reuses="ws_raw")
+        nc.sync.dma_start(w3_raw[:], words_of(w3_words))
+        place_scales(w3_s, ws_dealt, UPPER)
 
         w1_b = sb("w1_b", [P, PACK, P, PACK], BF16)
         w1_r = [w1_raw[u][:].rearrange("p j (m t) -> p t m j", t=PACK) for u in range(2)]
+        w1_c = sb("w1_c", [P, H], U32)
+        w1_s = sb("w1_s", [P, H], U8)
 
         def quant(codes, scales, src):
             nc.vector.quantize_mx(out=codes.bitcast(FP8X4), scales=scales, in_=src.rearrange("p s t -> p (s t)"))
@@ -116,21 +124,14 @@ def tile_picked_swapgate_sigmoid_po_kernel(
 
         for copy, ms in ((nc.vector.tensor_copy, slice(0, VECTOR_SHARE)), (nc.scalar.copy, slice(VECTOR_SHARE, P))):
             copy(w1_b[:, :, ms, 0:2].rearrange("p t m j -> p m t j"), w1_r[0][:, :, ms].rearrange("p t m j -> p m t j"))
-
-        def round_rest(i, copy):
-            copy(w1_b[:, PLANE[i], :, 2:PACK], w1_r[1][:, PLANE[i]])
-
         for copy, ms in ((nc.vector.tensor_copy, slice(0, P // 2)), (nc.scalar.copy, slice(P // 2, P))):
             copy(w1_b[:, PLANE[0], ms, 2:PACK], w1_r[1][:, PLANE[0], ms])
-        round_rest(1, nc.vector.tensor_copy)
-        for i in (2, 3):
-            round_rest(i, nc.scalar.copy)
-
-        w3_raw = sb("w3_raw", [P, N], I32, reuses="w1_raw0")
-        nc.sync.dma_start(w3_raw[:], words_of(w3_words))
-        w3_s_raw = sb("w3_s_raw", [P, N], U8, reuses="xw")
-        nc.gpsimd.memset(w3_s_raw[:].bitcast(I32), 0)
-        load_scales(nc.sync, w3_s_raw, w3_scales, range(4))
+        planes = list(PLANE)
+        nc.vector.tensor_copy(w1_b[:, planes[1], :, 2:PACK], w1_r[1][:, planes[1]])
+        for t in planes[2:]:
+            nc.scalar.copy(w1_b[:, t, :, 2:PACK], w1_r[1][:, t])
+        for t in planes:
+            quant(w1_c[:, plane_cols(t)], w1_s[:, plane_cols(t)], w1_b[:, t])
 
         def mm(dst, weights, weight_scales, moving, moving_scales):
             nc.tensor.matmul_mx(
@@ -143,34 +144,21 @@ def tile_picked_swapgate_sigmoid_po_kernel(
                 stop=True,
             )
 
-        w1_c, w1_s, y, pre, y_banks, gate_banks = {}, {}, {}, {}, {}, {}
+        y, pre, y_banks, gate_banks = {}, {}, {}, {}
         a, b, q, e, d, minus_d, z = {}, {}, {}, {}, {}, {}, {}
-        w2_c = {}
-
-        def deal_planes(into, name, raw, dtype, run, planes, reuses=None):
-            dealt = sb(name, [P, len(planes), P], dtype, reuses)
-            for j, t in enumerate(planes):
-                into[t] = dealt[:, j, :]
-            source = raw[:].rearrange("p (b i t) -> p b t i", t=PACK, i=run)
-            nc.vector.tensor_copy(dealt[:].rearrange("p t (b i) -> p b t i", i=run), source[:, :, planes.start : planes.stop, :])
-
+        w2_c = sb("w2_c", [P, H], I32)
         halves = (slice(0, S // 2), slice(S // 2, S))
         chunks = [slice(c, c + CHUNK) for c in range(0, S, CHUNK)]
         whole = slice(0, S)
 
-        def quant_w1(i, codes):
-            w1_c[i] = codes
-            w1_s[i] = sb("w1_s%d" % i, [P, P], U8)
-            quant(w1_c[i][:], w1_s[i][:], w1_b[:, PLANE[i]])
-
         def multiply_y(i, cols, number):
             acc = bank(number, [P, cols.stop - cols.start])
-            mm(acc[:], w1_c[i][:], w1_s[i][:], gw[:, cols], gs[:, cols])
+            mm(acc[:], w1_c[:, plane_cols(PLANE[i])], w1_s[:, plane_cols(PLANE[i])], gw[:, cols], gs[:, cols])
             return acc
 
         def multiply_gate(i, cols, number):
             acc = bank(number, [P, cols.stop - cols.start])
-            mm(acc[:], w2_c[PLANE[i]], ws_dealt[:, plane_cols(PLANE[i])], gw[:, cols], gs[:, cols])
+            mm(acc[:], w2_c[:, plane_cols(PLANE[i])], w2_s[:, plane_cols(PLANE[i])], gw[:, cols], gs[:, cols])
             return acc
 
         def empty(dst, acc):
@@ -180,11 +168,10 @@ def tile_picked_swapgate_sigmoid_po_kernel(
         def short(name, i, reuses=None):
             return sb("%s%d" % (name, i), [P, V], F32, reuses)
 
-        def get_ab(i, reuses=None):
-            both = sb("ab%d" % i, [P, 2, V], F32, reuses)
-            a[i], b[i] = both[:, 0, :], both[:, 1, :]
-            nc.scalar.activation(a[i], y[i][:].indirect(la_t[:]), ACT.Copy)
-            nc.scalar.activation(b[i], y[i][:].indirect(lb_t[:]), ACT.Copy)
+        def get_ab(i, tiles):
+            a[i], b[i] = tiles
+            nc.scalar.activation(a[i][:], y[i][:].indirect(la_t[:]), ACT.Copy)
+            nc.scalar.activation(b[i][:], y[i][:].indirect(lb_t[:]), ACT.Copy)
 
         def get_q(i, tile=None):
             q[i] = short("q", i) if tile is None else tile
@@ -198,8 +185,8 @@ def tile_picked_swapgate_sigmoid_po_kernel(
             d[i] = short("d", i)
             nc.vector.tensor_tensor(d[i][:], q[i][:], e[i][:], ALU.mult)
 
-        def negate_d(i, offset=None):
-            minus_d[i] = short("minus_d", i) if offset is None else at("minus_d%d" % i, [P, V], F32, offset)
+        def negate_d(i, reuses=None):
+            minus_d[i] = short("minus_d", i, reuses)
             nc.scalar.activation(minus_d[i][:], d[i][:], ACT.Copy, scale=-1.0)
 
         def put_na(i):
@@ -214,111 +201,100 @@ def tile_picked_swapgate_sigmoid_po_kernel(
             for c, copy in enumerate(copies):
                 copy(z_b[:, n * c : n * c + n, PLANE[i] : PLANE[i] + 2], pair[:, n * c : n * c + n, :])
 
-        quant_w1(0, sb("w1_c0", [P, P], U32))
-        ws_dealt = sb("ws_dealt", [P, H], U8, reuses="gs_raw")
-        deal(ws_dealt, ws_raw, LINE_BYTES)
-        deal_planes(w2_c, "w2_first", w2_raw, I32, LINE_WORDS, range(3, 4))
-        deal_planes(w2_c, "w2_rest", w2_raw, I32, LINE_WORDS, range(3))
-        quant_w1(1, at("w1_c1", [P, P], U32, 5 * ROW_BYTES))
-        y[0] = sb("y0", [P, S], F32)
-        for number, (copy, cols) in enumerate(zip((nc.scalar.copy, nc.scalar.copy, nc.scalar.copy), (halves[0], chunks[2], chunks[3]))):
-            copy(y[0][:, cols], multiply_y(0, cols, number)[:])
-        pre[0] = at("pre0", [P, S], F32, BASE + 64 - ROW_BYTES)
-        for cols, number in zip(halves, (3, 4)):
-            nc.scalar.copy(pre[0][:, cols], multiply_gate(0, cols, number)[:])
-        a[0] = at("a0", [P, V], F32, 5 * ROW_BYTES + 512)
-        e[0] = short("e", 0)
-        for v in (0, V // 2):
-            nc.vector.tensor_copy(a[0][:, v : v + V // 2], y[0][:].indirect(la_t[:, v // LIST : (v + V // 2) // LIST]))
-        for v in (0, V // 2):
-            window = y[0][:].indirect(lb_t[:, v // LIST : (v + V // 2) // LIST])
-            nc.vector.tensor_tensor(e[0][:, v : v + V // 2], window, a[0][:, v : v + V // 2], ALU.subtract)
-        y1_banks = [multiply_y(1, cols, number) for cols, number in zip(halves, (5, 4))]
-        gate_banks[1] = multiply_gate(1, whole, 6)
-        quant_w1(2, sb("w1_c2", [P, P], U32, reuses="w2_first"))
-        y_banks[2] = [multiply_y(2, cols, number) for cols, number in zip(halves, (7, 5))]
-        get_q(0)
-        get_d(0)
-        quant_w1(3, at("w1_c3", [P, P], U32, BASE + 64 - ROW_BYTES))
-        gate_banks[2] = multiply_gate(2, whole, 0)
-        y_banks[3] = [multiply_y(3, cols, number) for cols, number in zip(halves, (1, 3))]
-        gate_banks[3] = multiply_gate(3, whole, 2)
         na, nb = {}, {}
 
-        def two(engine, name, i, left, right, op, reuses=None):
-            out = short(name, i, reuses)
+        def two(engine, out, left, right, op):
             engine.tensor_tensor(out[:], left[:], right[:], op)
             return out
 
         def put(i, offsets, values):
             nc.vector.tensor_copy(z[i][:].indirect(offsets[:]), values[:])
 
-        def on_gpsimd(i, sums=True, reuses=None):
-            e[i] = two(nc.gpsimd, "e", i, b[i], a[i], ALU.subtract, reuses)
-            get_q(i, q_tiles[i]())
-            d[i] = two(nc.gpsimd, "d", i, q[i], e[i], ALU.mult)
-            if sums:
-                na[i] = two(nc.gpsimd, "na", i, a[i], d[i], ALU.add)
-                nb[i] = two(nc.gpsimd, "nb", i, b[i], d[i], ALU.subtract)
+        def gather(i, offsets, out):
+            nc.vector.tensor_copy(out[:], y[i][:].indirect(offsets[:]))
+            return out
 
-        q_tiles = {
-            1: lambda: at("q1", [P, V], F32, BASE + 1088),
-            2: lambda: short("q", 2),
-            3: lambda: short("q", 3),
-        }
-        na[0] = two(nc.vector, "na", 0, a[0], d[0], ALU.add)
-        rest = two(nc.vector, "rest", 0, e[0], d[0], ALU.subtract)
+        y[0] = sb("y0", [P, S], F32)
+        for number, (copy, cols) in enumerate(zip((nc.scalar.copy, nc.scalar.copy, nc.vector.tensor_copy), (halves[0], chunks[2], chunks[3]))):
+            copy(y[0][:, cols], multiply_y(0, cols, number)[:])
+        deal(w2_c, w2_raw, LINE_WORDS)
+        for i in (1, 2, 3):
+            y_banks[i] = multiply_y(i, whole, 2 + i)
+        y[1] = sb("y1", [P, S], F32)
+        empty(y[1], y_banks[1])
+        a[0] = gather(0, la_t, short("a", 0))
+        b[0] = short("b", 0)
+        nc.scalar.activation(b[0][:], y[0][:].indirect(lb_t[:]), ACT.Copy)
+        a[1] = gather(1, la_t, short("a", 1))
+        b[1] = gather(1, lb_t, short("b", 1))
+        get_e(0)
+        get_e(1)
+        pre[0] = at("pre0", [P, S], F32, 0)
+        for cols, number in zip(halves, (6, 7)):
+            nc.scalar.copy(pre[0][:, cols], multiply_gate(0, cols, number)[:])
+        for i in (1, 2, 3):
+            gate_banks[i] = multiply_gate(i, whole, (0, 0, 1, 2)[i])
+        get_q(0)
+        pre[1] = at("pre1", [P, S], F32, 2 * ROW_BYTES)
+        empty(pre[1], gate_banks[1])
+        get_q(1)
+
+        get_d(0)
+        y[2] = at("y2", [P, S], F32, 0)
+        nc.vector.tensor_copy(y[2][:, halves[0]], y_banks[2][:, halves[0]])
+        na[0] = two(nc.vector, short("na", 0), a[0], d[0], ALU.add)
+        nc.vector.tensor_copy(y[2][:, halves[1]], y_banks[2][:, halves[1]])
         z[0] = sb("z0", [P, S], F32)
         put(0, la_t, na[0])
-        nb[0] = two(nc.gpsimd, "nb", 0, a[0], rest, ALU.add)
 
-        y[1] = at("y1", [P, S], F32, BASE + 64)
-        for cols, acc in zip(halves, y1_banks):
-            nc.scalar.copy(y[1][:, cols], acc[:])
-        get_ab(1)
-        pre[1] = sb("pre1", [P, S], F32)
-        empty(pre[1], gate_banks[1])
-        y[2] = sb("y2", [P, S], F32, reuses="rest0")
-        nc.vector.tensor_copy(y[2][:, halves[0]], y_banks[2][0][:])
-        put(0, lb_t, nb[0])
-        z[2] = sb("z2", [P, 2 * S], F32)
-        nc.sync.dma_start(z[2][:, S : 2 * S], z[0][:])
-        on_gpsimd(1, reuses="e0")
+        d[1] = two(nc.gpsimd, short("d", 1), q[1], e[1], ALU.mult)
+        na[1] = two(nc.gpsimd, short("na", 1), a[1], d[1], ALU.add)
         z[1] = sb("z1", [P, S], F32)
         put(1, la_t, na[1])
-
-        nc.scalar.copy(y[2][:, halves[1]], y_banks[2][1][:])
-        get_ab(2, reuses="pre1")
-        pre[2] = sb("pre2", [P, S], F32)
-        empty(pre[2], gate_banks[2])
-        y[3] = sb("y3", [P, S], F32, reuses="d1")
-        nc.vector.tensor_copy(y[3][:, halves[0]], y_banks[3][0][:])
+        nb[0] = two(nc.gpsimd, short("nb", 0, reuses="a1"), b[0], d[0], ALU.subtract)
+        put(0, lb_t, nb[0])
+        nb[1] = two(nc.gpsimd, short("nb", 1), b[1], d[1], ALU.subtract)
         put(1, lb_t, nb[1])
-        on_gpsimd(2, reuses="ab1")
-        put(2, la_t, na[2])
-        put(2, lb_t, nb[2])
 
-        pre[3] = sb("pre3", [P, S], F32)
+        get_ab(2, (short("a", 2), short("b", 2)))
+        pre[2] = at("pre2", [P, S], F32, ROW_BYTES + 64)
+        empty(pre[2], gate_banks[2])
+        get_q(2)
+        e[2] = two(nc.gpsimd, short("e", 2, reuses="b1"), b[2], a[2], ALU.subtract)
+        d[2] = two(nc.gpsimd, short("d", 2), q[2], e[2], ALU.mult)
+        na[2] = two(nc.gpsimd, short("na", 2), a[2], d[2], ALU.add)
+        y[3] = at("y3", [P, S], F32, 2 * ROW_BYTES + 64)
+        empty(y[3], y_banks[3])
+        pre[3] = at("pre3", [P, S], F32, 64)
         empty(pre[3], gate_banks[3])
-        nc.scalar.copy(y[3][:, halves[1]], y_banks[3][1][:])
-        get_ab(3, reuses="pre2")
-        on_gpsimd(3, sums=False, reuses="pre1")
-        z[3] = sb("z3", [P, 2 * S], F32, reuses="pre3")
-        nc.scalar.copy(z[3][:, S : 2 * S], z[1][:])
+        get_ab(3, (short("a", 3), short("b", 3)))
+        get_q(3)
+        z[2] = at("z2", [P, 2 * S], F32, 2 * ROW_BYTES + 64)
+        put(2, la_t, na[2])
+        e[3] = two(nc.gpsimd, short("e", 3, reuses="a2"), b[3], a[3], ALU.subtract)
+        d[3] = two(nc.gpsimd, short("d", 3), q[3], e[3], ALU.mult)
+        z[3] = sb("z3", [P, 2 * S], F32)
         put_na(3)
+        negate_d(2, reuses="q3")
+        nc.scalar.copy(z[2][:, S : 2 * S], z[0][:])
+        put_nb(2)
         negate_d(3)
-        z_b = sb("z_b", [P, S, PACK], BF16, reuses="q3")
-        weave(2, [nc.scalar.copy])
+        nc.scalar.copy(z[3][:, S : 2 * S], z[1][:])
 
-        w3_dealt = sb("w3_dealt", [P, N], I32, reuses="pre1")
-        deal(w3_dealt, w3_raw, LINE_WORDS)
-        w3_c = [w3_dealt[:, plane_cols(t)] for t in range(PACK)]
-        idle = bank(3, [P, S])
+        def deal_w3(copy, dtype, name, planes, reuses):
+            dealt = sb(name, [P, len(planes), P], dtype, reuses)
+            source = w3_raw[:].bitcast(dtype).rearrange("p (b i t) -> p b t i", t=PACK, i=LINE_WORDS)
+            copy(dealt[:].rearrange("p t (b i) -> p b t i", i=LINE_WORDS), source[:, :, planes.start : planes.stop, :])
+            return [dealt[:, j, :] for j in range(len(planes))]
+
+        w3_c = deal_w3(nc.scalar.copy, U32, "w3_rest", range(1, PACK), "z0")
+        w3_c = deal_w3(nc.vector.tensor_copy, I32, "w3_first", range(1), "d2") + w3_c
+        z_b = sb("z_b", [P, S, PACK], BF16)
+        weave(2, [nc.scalar.copy])
+        idle = bank(4, [P, S])
         for warm_pass in range(WARM_PASSES):
-            mm(idle[:], w3_c[0], ws_dealt[:, plane_cols(0)], gw[:], gs[:])
+            mm(idle[:], w3_c[0], w3_s[:, plane_cols(0)], gw[:], gs[:])
         put_nb(3)
-        w3_s = sb("w3_s", [P, N], U8, reuses="d3")
-        deal(w3_s, w3_s_raw, LINE_BYTES)
         weave(3, [nc.vector.tensor_copy] * 2 + [nc.scalar.copy] * 2)
 
         z_s = sb("z_s", [P, S], U8)
@@ -333,7 +309,7 @@ def tile_picked_swapgate_sigmoid_po_kernel(
         for cols in chunks:
             quant(z_c[:, cols], z_s[:, cols], z_b[:, cols, :])
         def multiply_out(c, planes):
-            acc = bank((4 + 2 * c + planes[0] // 2) % 8, [P, len(planes), CHUNK])
+            acc = bank((5 + 2 * c + planes[0] // 2) % 8, [P, len(planes), CHUNK])
             for j, t in enumerate(planes):
                 mm(acc[:, j, :], w3_c[t], w3_s[:, plane_cols(t)], z_c[:, chunks[c]], z_s[:, chunks[c]])
             return acc

@@ -220,26 +220,35 @@ def tile_picked_swapgate_sigmoid_po_kernel(
         deal(w2_c, w2_raw, LINE_WORDS)
         for i in (1, 2, 3):
             y_banks[i] = multiply_y(i, whole, 2 + i)
+        def pair(name, reuses=None):
+            return sb(name, [P, 2, V], F32, reuses)
+
+        def fetch(out, window, offsets, func=ACT.Copy):
+            nc.scalar.activation(out, window[:].indirect(offsets[:]), func)
+
         y[1] = sb("y1", [P, S], F32)
         empty(y[1], y_banks[1])
-        a[0] = gather(0, la_t, short("a", 0))
-        b[0] = short("b", 0)
-        nc.scalar.activation(b[0][:], y[0][:].indirect(lb_t[:]), ACT.Copy)
-        a[1] = gather(1, la_t, short("a", 1))
-        b[1] = gather(1, lb_t, short("b", 1))
+        b_early, d_early = pair("b_early"), pair("d_early")
+        for i in range(2):
+            a[i], b[i], d[i] = short("a", i), b_early[:, i, :], d_early[:, i, :]
+        gather(0, la_t, a[0])
+        fetch(b[0], y[0], lb_t)
+        gather(1, la_t, a[1])
+        gather(1, lb_t, b[1])
         get_e(0)
         get_e(1)
         pre[0] = at("pre0", [P, S], F32, 0)
         for cols, number in zip(halves, (6, 7)):
             nc.scalar.copy(pre[0][:, cols], multiply_gate(0, cols, number)[:])
-        for i in (1, 2, 3):
-            gate_banks[i] = multiply_gate(i, whole, (0, 0, 1, 2)[i])
+        for i in (1, 2):
+            gate_banks[i] = multiply_gate(i, whole, i - 1)
+        gate_banks[3] = [multiply_gate(3, cols, number) for cols, number in zip(halves, (2, 3))]
         get_q(0)
         pre[1] = at("pre1", [P, S], F32, 2 * ROW_BYTES)
         empty(pre[1], gate_banks[1])
         get_q(1)
 
-        get_d(0)
+        two(nc.vector, d[0], q[0], e[0], ALU.mult)
         y[2] = at("y2", [P, S], F32, 0)
         nc.vector.tensor_copy(y[2][:, halves[0]], y_banks[2][:, halves[0]])
         na[0] = two(nc.vector, short("na", 0), a[0], d[0], ALU.add)
@@ -247,39 +256,39 @@ def tile_picked_swapgate_sigmoid_po_kernel(
         z[0] = sb("z0", [P, S], F32)
         put(0, la_t, na[0])
 
-        d[1] = two(nc.gpsimd, short("d", 1), q[1], e[1], ALU.mult)
+        two(nc.gpsimd, d[1], q[1], e[1], ALU.mult)
         na[1] = two(nc.gpsimd, short("na", 1), a[1], d[1], ALU.add)
+        pre[3] = sb("pre3", [P, S], F32, reuses="q1")
+        nc.vector.tensor_copy(pre[3][:, halves[0]], gate_banks[3][0][:])
         z[1] = sb("z1", [P, S], F32)
         put(1, la_t, na[1])
-        nb[0] = two(nc.gpsimd, short("nb", 0, reuses="a1"), b[0], d[0], ALU.subtract)
-        put(0, lb_t, nb[0])
-        nb[1] = two(nc.gpsimd, short("nb", 1), b[1], d[1], ALU.subtract)
-        put(1, lb_t, nb[1])
+        nb_early = two(nc.gpsimd, pair("nb_early", reuses="a1"), b_early, d_early, ALU.subtract)
+        for i in range(2):
+            put(i, lb_t, nb_early[:, i, :])
 
-        get_ab(2, (short("a", 2), short("b", 2)))
+        a_late, b_late, q_late = pair("a_late"), pair("b_late"), pair("q_late")
+        y[3] = at("y3", [P, S], F32, 2 * ROW_BYTES + 64)
+        for i in (2, 3):
+            a[i], b[i] = a_late[:, i - 2, :], b_late[:, i - 2, :]
+            if i == 3:
+                empty(y[3], y_banks[3])
+            fetch(a[i], y[i], la_t)
+            fetch(b[i], y[i], lb_t)
         pre[2] = at("pre2", [P, S], F32, ROW_BYTES + 64)
         empty(pre[2], gate_banks[2])
-        get_q(2)
-        e[2] = two(nc.gpsimd, short("e", 2, reuses="b1"), b[2], a[2], ALU.subtract)
-        d[2] = two(nc.gpsimd, short("d", 2), q[2], e[2], ALU.mult)
-        na[2] = two(nc.gpsimd, short("na", 2), a[2], d[2], ALU.add)
-        y[3] = at("y3", [P, S], F32, 2 * ROW_BYTES + 64)
-        empty(y[3], y_banks[3])
-        pre[3] = at("pre3", [P, S], F32, 64)
-        empty(pre[3], gate_banks[3])
-        get_ab(3, (short("a", 3), short("b", 3)))
-        get_q(3)
-        z[2] = at("z2", [P, 2 * S], F32, 2 * ROW_BYTES + 64)
-        put(2, la_t, na[2])
-        e[3] = two(nc.gpsimd, short("e", 3, reuses="a2"), b[3], a[3], ALU.subtract)
-        d[3] = two(nc.gpsimd, short("d", 3), q[3], e[3], ALU.mult)
-        z[3] = sb("z3", [P, 2 * S], F32)
-        put_na(3)
-        negate_d(2, reuses="q3")
-        nc.scalar.copy(z[2][:, S : 2 * S], z[0][:])
+        nc.scalar.copy(pre[3][:, halves[1]], gate_banks[3][1][:])
+        for i in (2, 3):
+            fetch(q_late[:, i - 2, :], pre[i], la_t, ACT.Sigmoid)
+        e_late = two(nc.gpsimd, pair("e_late", reuses="b_early"), b_late, a_late, ALU.subtract)
+        d_late = two(nc.gpsimd, pair("d_late"), q_late, e_late, ALU.mult)
+        minus_late = pair("minus_late")
+        nc.scalar.activation(minus_late[:], d_late[:], ACT.Copy, scale=-1.0)
+        for i in (2, 3):
+            d[i], minus_d[i] = d_late[:, i - 2, :], minus_late[:, i - 2, :]
+            z[i] = sb("z%d" % i, [P, 2 * S], F32)
+            put_na(i)
+            nc.scalar.copy(z[i][:, S : 2 * S], z[i - 2][:])
         put_nb(2)
-        negate_d(3)
-        nc.scalar.copy(z[3][:, S : 2 * S], z[1][:])
 
         def deal_w3(copy, dtype, name, planes, reuses):
             dealt = sb(name, [P, len(planes), P], dtype, reuses)
@@ -287,8 +296,8 @@ def tile_picked_swapgate_sigmoid_po_kernel(
             copy(dealt[:].rearrange("p t (b i) -> p b t i", i=LINE_WORDS), source[:, :, planes.start : planes.stop, :])
             return [dealt[:, j, :] for j in range(len(planes))]
 
-        w3_c = deal_w3(nc.scalar.copy, U32, "w3_rest", range(1, PACK), "z0")
-        w3_c = deal_w3(nc.vector.tensor_copy, I32, "w3_first", range(1), "d2") + w3_c
+        w3_c = deal_w3(nc.scalar.copy, U32, "w3_rest", range(1, PACK), "q_late")
+        w3_c = deal_w3(nc.vector.tensor_copy, I32, "w3_first", range(1), "z0") + w3_c
         z_b = sb("z_b", [P, S, PACK], BF16)
         weave(2, [nc.scalar.copy])
         idle = bank(4, [P, S])

@@ -266,7 +266,7 @@ def tile_picked_swapgate_sigmoid_po_kernel(
         for i in range(2):
             put(i, lb_t, nb_early[:, i, :])
 
-        a_late, b_late, q_late = pair("a_late"), pair("b_late"), pair("q_late")
+        a_late, b_late = pair("a_late"), pair("b_late")
         y[3] = at("y3", [P, S], F32, 2 * ROW_BYTES + 64)
         for i in (2, 3):
             a[i], b[i] = a_late[:, i - 2, :], b_late[:, i - 2, :]
@@ -278,13 +278,13 @@ def tile_picked_swapgate_sigmoid_po_kernel(
         empty(pre[2], gate_banks[2])
         nc.scalar.copy(pre[3][:, halves[1]], gate_banks[3][1][:])
         for i in (2, 3):
-            fetch(q_late[:, i - 2, :], pre[i], la_t, ACT.Sigmoid)
+            get_q(i)
         e_late = two(nc.gpsimd, pair("e_late", reuses="b_early"), b_late, a_late, ALU.subtract)
-        d_late = two(nc.gpsimd, pair("d_late"), q_late, e_late, ALU.mult)
-        minus_late = pair("minus_late")
-        nc.scalar.activation(minus_late[:], d_late[:], ACT.Copy, scale=-1.0)
+        d[2] = two(nc.gpsimd, short("d", 2), q[2], e_late[:, 0, :], ALU.mult)
+        d[3] = two(nc.vector, short("d", 3, reuses="q2"), q[3], e_late[:, 1, :], ALU.mult)
         for i in (2, 3):
-            d[i], minus_d[i] = d_late[:, i - 2, :], minus_late[:, i - 2, :]
+            negate_d(i)
+        for i in (2, 3):
             z[i] = sb("z%d" % i, [P, 2 * S], F32)
             put_na(i)
             nc.scalar.copy(z[i][:, S : 2 * S], z[i - 2][:])
@@ -296,9 +296,9 @@ def tile_picked_swapgate_sigmoid_po_kernel(
             copy(dealt[:].rearrange("p t (b i) -> p b t i", i=LINE_WORDS), source[:, :, planes.start : planes.stop, :])
             return [dealt[:, j, :] for j in range(len(planes))]
 
-        w3_c = deal_w3(nc.scalar.copy, U32, "w3_rest", range(1, PACK), "q_late")
-        w3_c = deal_w3(nc.vector.tensor_copy, I32, "w3_first", range(1), "z0") + w3_c
-        z_b = sb("z_b", [P, S, PACK], BF16)
+        w3_c = deal_w3(nc.scalar.copy, U32, "w3_rest", range(1, PACK), "q3")
+        w3_c = deal_w3(nc.scalar.copy, U32, "w3_first", range(1), "z1") + w3_c
+        z_b = sb("z_b", [P, S, PACK], BF16, reuses="ws_raw")
         weave(2, [nc.scalar.copy])
         idle = bank(4, [P, S])
         for warm_pass in range(WARM_PASSES):

@@ -218,8 +218,7 @@ def tile_picked_swapgate_sigmoid_po_kernel(
         for number, (copy, cols) in enumerate(zip((nc.scalar.copy, nc.scalar.copy, nc.vector.tensor_copy), (halves[0], chunks[2], chunks[3]))):
             copy(y[0][:, cols], multiply_y(0, cols, number)[:])
         deal(w2_c, w2_raw, LINE_WORDS)
-        for i in (1, 2, 3):
-            y_banks[i] = multiply_y(i, whole, 2 + i)
+        y_banks[1] = multiply_y(1, whole, 3)
         def pair(name, reuses=None):
             return sb(name, [P, 2, V], F32, reuses)
 
@@ -228,11 +227,10 @@ def tile_picked_swapgate_sigmoid_po_kernel(
 
         y[1] = sb("y1", [P, S], F32)
         empty(y[1], y_banks[1])
-        b_early, d_early = pair("b_early"), pair("d_early")
         for i in range(2):
-            a[i], b[i], d[i] = short("a", i), b_early[:, i, :], d_early[:, i, :]
+            a[i], b[i] = short("a", i), short("b", i)
         gather(0, la_t, a[0])
-        fetch(b[0], y[0], lb_t)
+        fetch(b[0][:], y[0], lb_t)
         gather(1, la_t, a[1])
         gather(1, lb_t, b[1])
         get_e(0)
@@ -240,15 +238,18 @@ def tile_picked_swapgate_sigmoid_po_kernel(
         pre[0] = at("pre0", [P, S], F32, 0)
         for cols, number in zip(halves, (6, 7)):
             nc.scalar.copy(pre[0][:, cols], multiply_gate(0, cols, number)[:])
-        for i in (1, 2):
-            gate_banks[i] = multiply_gate(i, whole, i - 1)
-        gate_banks[3] = [multiply_gate(3, cols, number) for cols, number in zip(halves, (2, 3))]
+        gate_banks[1] = [multiply_gate(1, cols, number) for cols, number in zip(halves, (1, 7))]
+        y_banks[2] = multiply_y(2, whole, 6)
+        gate_banks[2] = multiply_gate(2, whole, 2)
+        gate_banks[3] = [multiply_gate(3, cols, number) for cols, number in zip(halves, (4, 5))]
         get_q(0)
         pre[1] = at("pre1", [P, S], F32, 2 * ROW_BYTES)
-        empty(pre[1], gate_banks[1])
+        for cols, acc in zip(halves, gate_banks[1]):
+            nc.scalar.copy(pre[1][:, cols], acc[:])
         get_q(1)
+        y_banks[3] = [multiply_y(3, cols, number) for cols, number in zip(halves, (1, 7))]
 
-        two(nc.vector, d[0], q[0], e[0], ALU.mult)
+        get_d(0)
         y[2] = at("y2", [P, S], F32, 0)
         nc.vector.tensor_copy(y[2][:, halves[0]], y_banks[2][:, halves[0]])
         na[0] = two(nc.vector, short("na", 0), a[0], d[0], ALU.add)
@@ -256,22 +257,24 @@ def tile_picked_swapgate_sigmoid_po_kernel(
         z[0] = sb("z0", [P, S], F32)
         put(0, la_t, na[0])
 
-        two(nc.gpsimd, d[1], q[1], e[1], ALU.mult)
+        nb[0] = two(nc.gpsimd, short("nb", 0, reuses="a0"), b[0], d[0], ALU.subtract)
+        y[3] = sb("y3", [P, S], F32, reuses="b0")
+        nc.vector.tensor_copy(y[3][:, halves[0]], y_banks[3][0][:])
+        put(0, lb_t, nb[0])
+        d[1] = two(nc.gpsimd, short("d", 1, reuses="d0"), q[1], e[1], ALU.mult)
         na[1] = two(nc.gpsimd, short("na", 1), a[1], d[1], ALU.add)
-        pre[3] = sb("pre3", [P, S], F32, reuses="q1")
-        nc.vector.tensor_copy(pre[3][:, halves[0]], gate_banks[3][0][:])
         z[1] = sb("z1", [P, S], F32)
         put(1, la_t, na[1])
-        nb_early = two(nc.gpsimd, pair("nb_early", reuses="a1"), b_early, d_early, ALU.subtract)
-        for i in range(2):
-            put(i, lb_t, nb_early[:, i, :])
+        nb[1] = two(nc.gpsimd, short("nb", 1, reuses="a1"), b[1], d[1], ALU.subtract)
+        pre[3] = sb("pre3", [P, S], F32, reuses="b1")
+        nc.vector.tensor_copy(pre[3][:, halves[0]], gate_banks[3][0][:])
+        put(1, lb_t, nb[1])
 
         a_late, b_late = pair("a_late"), pair("b_late")
-        y[3] = at("y3", [P, S], F32, 2 * ROW_BYTES + 64)
         for i in (2, 3):
             a[i], b[i] = a_late[:, i - 2, :], b_late[:, i - 2, :]
             if i == 3:
-                empty(y[3], y_banks[3])
+                nc.scalar.copy(y[3][:, halves[1]], y_banks[3][1][:])
             fetch(a[i], y[i], la_t)
             fetch(b[i], y[i], lb_t)
         pre[2] = at("pre2", [P, S], F32, ROW_BYTES + 64)
@@ -279,7 +282,7 @@ def tile_picked_swapgate_sigmoid_po_kernel(
         nc.scalar.copy(pre[3][:, halves[1]], gate_banks[3][1][:])
         for i in (2, 3):
             get_q(i)
-        e_late = two(nc.gpsimd, pair("e_late", reuses="b_early"), b_late, a_late, ALU.subtract)
+        e_late = two(nc.gpsimd, pair("e_late", reuses="d0"), b_late, a_late, ALU.subtract)
         d[2] = two(nc.gpsimd, short("d", 2), q[2], e_late[:, 0, :], ALU.mult)
         d[3] = two(nc.vector, short("d", 3, reuses="q2"), q[3], e_late[:, 1, :], ALU.mult)
         for i in (2, 3):
@@ -300,7 +303,7 @@ def tile_picked_swapgate_sigmoid_po_kernel(
         w3_c = deal_w3(nc.scalar.copy, U32, "w3_first", range(1), "z1") + w3_c
         z_b = sb("z_b", [P, S, PACK], BF16, reuses="ws_raw")
         weave(2, [nc.scalar.copy])
-        idle = bank(4, [P, S])
+        idle = bank(0, [P, S])
         for warm_pass in range(WARM_PASSES):
             mm(idle[:], w3_c[0], w3_s[:, plane_cols(0)], gw[:], gs[:])
         put_nb(3)
@@ -318,7 +321,7 @@ def tile_picked_swapgate_sigmoid_po_kernel(
         for cols in chunks:
             quant(z_c[:, cols], z_s[:, cols], z_b[:, cols, :])
         def multiply_out(c, planes):
-            acc = bank((5 + 2 * c + planes[0] // 2) % 8, [P, len(planes), CHUNK])
+            acc = bank((1 + 2 * c + planes[0] // 2) % 8, [P, len(planes), CHUNK])
             for j, t in enumerate(planes):
                 mm(acc[:, j, :], w3_c[t], w3_s[:, plane_cols(t)], z_c[:, chunks[c]], z_s[:, chunks[c]])
             return acc

@@ -239,7 +239,7 @@ def tile_picked_swapgate_sigmoid_po_kernel(
         for cols, number in zip(halves, (6, 7)):
             nc.scalar.copy(pre[0][:, cols], multiply_gate(0, cols, number)[:])
         gate_banks[1] = [multiply_gate(1, cols, number) for cols, number in zip(halves, (1, 7))]
-        y_banks[2] = multiply_y(2, whole, 6)
+        y_banks[2] = [multiply_y(2, halves[0], 6)]
         gate_banks[2] = multiply_gate(2, whole, 2)
         gate_banks[3] = [multiply_gate(3, cols, number) for cols, number in zip(halves, (4, 5))]
         get_q(0)
@@ -247,17 +247,17 @@ def tile_picked_swapgate_sigmoid_po_kernel(
         for cols, acc in zip(halves, gate_banks[1]):
             nc.scalar.copy(pre[1][:, cols], acc[:])
         get_q(1)
-        y_banks[3] = [multiply_y(3, cols, number) for cols, number in zip(halves, (1, 7))]
+        y_banks[2].append(multiply_y(2, halves[1], 1))
 
         get_d(0)
         y[2] = at("y2", [P, S], F32, 0)
-        nc.vector.tensor_copy(y[2][:, halves[0]], y_banks[2][:, halves[0]])
+        nc.vector.tensor_copy(y[2][:, halves[0]], y_banks[2][0][:])
         na[0] = two(nc.vector, short("na", 0), a[0], d[0], ALU.add)
-        nc.vector.tensor_copy(y[2][:, halves[1]], y_banks[2][:, halves[1]])
+        y_banks[3] = [multiply_y(3, cols, number) for cols, number in zip(halves, (7, 6))]
+        nb[0] = two(nc.vector, short("nb", 0), b[0], d[0], ALU.subtract)
         z[0] = sb("z0", [P, S], F32)
         put(0, la_t, na[0])
 
-        nb[0] = two(nc.gpsimd, short("nb", 0, reuses="a0"), b[0], d[0], ALU.subtract)
         y[3] = sb("y3", [P, S], F32, reuses="b0")
         nc.vector.tensor_copy(y[3][:, halves[0]], y_banks[3][0][:])
         put(0, lb_t, nb[0])
@@ -273,8 +273,7 @@ def tile_picked_swapgate_sigmoid_po_kernel(
         a_late, b_late = pair("a_late"), pair("b_late")
         for i in (2, 3):
             a[i], b[i] = a_late[:, i - 2, :], b_late[:, i - 2, :]
-            if i == 3:
-                nc.scalar.copy(y[3][:, halves[1]], y_banks[3][1][:])
+            nc.scalar.copy(y[i][:, halves[1]], y_banks[i][1][:])
             fetch(a[i], y[i], la_t)
             fetch(b[i], y[i], lb_t)
         pre[2] = at("pre2", [P, S], F32, ROW_BYTES + 64)

@@ -29,7 +29,7 @@ LINE_BYTES = 16
 VECTOR_SHARE = 80
 WARM_PASSES = 3
 
-PLANE = (1, 3, 0, 2)
+PLANE = (3, 1, 2, 0)
 
 
 def words_of(packed):
@@ -146,7 +146,6 @@ def tile_picked_swapgate_sigmoid_po_kernel(
 
         y, pre, y_banks, gate_banks = {}, {}, {}, {}
         a, b, q, e, d, minus_d, z = {}, {}, {}, {}, {}, {}, {}
-        w2_c = sb("w2_c", [P, H], I32)
         halves = (slice(0, S // 2), slice(S // 2, S))
         chunks = [slice(c, c + CHUNK) for c in range(0, S, CHUNK)]
         whole = slice(0, S)
@@ -158,7 +157,7 @@ def tile_picked_swapgate_sigmoid_po_kernel(
 
         def multiply_gate(i, cols, number):
             acc = bank(number, [P, cols.stop - cols.start])
-            mm(acc[:], w2_c[:, plane_cols(PLANE[i])], w2_s[:, plane_cols(PLANE[i])], gw[:, cols], gs[:, cols])
+            mm(acc[:], w2_c[PLANE[i]], w2_s[:, plane_cols(PLANE[i])], gw[:, cols], gs[:, cols])
             return acc
 
         def empty(dst, acc):
@@ -217,8 +216,14 @@ def tile_picked_swapgate_sigmoid_po_kernel(
         y[0] = sb("y0", [P, S], F32)
         for number, (copy, cols) in enumerate(zip((nc.scalar.copy, nc.scalar.copy, nc.vector.tensor_copy), (halves[0], chunks[2], chunks[3]))):
             copy(y[0][:, cols], multiply_y(0, cols, number)[:])
-        deal(w2_c, w2_raw, LINE_WORDS)
+        w2_planes = w2_raw[:].rearrange("p (b i t) -> p b t i", t=PACK, i=LINE_WORDS)
+        w2_first = at("w2_first", [P, P], I32, 5 * ROW_BYTES)
+        nc.vector.tensor_copy(w2_first[:].rearrange("p (b i) -> p b i", i=LINE_WORDS), w2_planes[:, :, PACK - 1, :])
+        w2_rest = sb("w2_rest", [P, PACK - 1, P], I32)
+        nc.vector.tensor_copy(w2_rest[:].rearrange("p t (b i) -> p b t i", i=LINE_WORDS), w2_planes[:, :, 0 : PACK - 1, :])
+        w2_c = [w2_rest[:, t, :] for t in range(PACK - 1)] + [w2_first[:]]
         y_banks[1] = multiply_y(1, whole, 3)
+        y_banks[2] = [multiply_y(2, cols, number) for cols, number in zip(halves, (4, 0))]
         def pair(name, reuses=None):
             return sb(name, [P, 2, V], F32, reuses)
 
@@ -227,33 +232,31 @@ def tile_picked_swapgate_sigmoid_po_kernel(
 
         y[1] = sb("y1", [P, S], F32)
         empty(y[1], y_banks[1])
-        for i in range(2):
-            a[i], b[i] = short("a", i), short("b", i)
+        a[0], a[1], b[0] = short("a", 0), short("a", 1), short("b", 0)
         gather(0, la_t, a[0])
         fetch(b[0][:], y[0], lb_t)
         gather(1, la_t, a[1])
-        gather(1, lb_t, b[1])
         get_e(0)
-        get_e(1)
         pre[0] = at("pre0", [P, S], F32, 0)
         for cols, number in zip(halves, (6, 7)):
-            nc.scalar.copy(pre[0][:, cols], multiply_gate(0, cols, number)[:])
+            nc.scalar.activation(pre[0][:, cols], multiply_gate(0, cols, number)[:], ACT.Sigmoid)
         gate_banks[1] = [multiply_gate(1, cols, number) for cols, number in zip(halves, (1, 7))]
-        y_banks[2] = [multiply_y(2, halves[0], 6)]
         gate_banks[2] = multiply_gate(2, whole, 2)
-        gate_banks[3] = [multiply_gate(3, cols, number) for cols, number in zip(halves, (4, 5))]
-        get_q(0)
+        gate_banks[3] = [multiply_gate(3, cols, number) for cols, number in zip(halves, (5, 3))]
+        b[1] = at("b1", [P, V], F32, 5 * ROW_BYTES + 256)
+        fetch(b[1][:], y[1], lb_t)
         pre[1] = at("pre1", [P, S], F32, 2 * ROW_BYTES)
         for cols, acc in zip(halves, gate_banks[1]):
             nc.scalar.copy(pre[1][:, cols], acc[:])
         get_q(1)
-        y_banks[2].append(multiply_y(2, halves[1], 1))
 
-        get_d(0)
-        y[2] = at("y2", [P, S], F32, 0)
+        y[2] = at("y2", [P, S], F32, 4 * ROW_BYTES + 256)
         nc.vector.tensor_copy(y[2][:, halves[0]], y_banks[2][0][:])
+        d[0] = short("d", 0)
+        nc.vector.tensor_tensor(d[0][:], pre[0][:].indirect(la_t[:]), e[0][:], ALU.mult)
+        get_e(1)
         na[0] = two(nc.vector, short("na", 0), a[0], d[0], ALU.add)
-        y_banks[3] = [multiply_y(3, cols, number) for cols, number in zip(halves, (7, 6))]
+        y_banks[3] = [multiply_y(3, cols, number) for cols, number in zip(halves, (6, 7))]
         nb[0] = two(nc.vector, short("nb", 0), b[0], d[0], ALU.subtract)
         z[0] = sb("z0", [P, S], F32)
         put(0, la_t, na[0])
@@ -266,7 +269,7 @@ def tile_picked_swapgate_sigmoid_po_kernel(
         z[1] = sb("z1", [P, S], F32)
         put(1, la_t, na[1])
         nb[1] = two(nc.gpsimd, short("nb", 1, reuses="a1"), b[1], d[1], ALU.subtract)
-        pre[3] = sb("pre3", [P, S], F32, reuses="b1")
+        pre[3] = at("pre3", [P, S], F32, 5 * ROW_BYTES + 256)
         nc.vector.tensor_copy(pre[3][:, halves[0]], gate_banks[3][0][:])
         put(1, lb_t, nb[1])
 

from contextlib import ExitStack

import concourse.mybir as mybir

K, T, S, V, N, H = 512, 2048, 512, 256, 512, 512
FLOPS = 2 * K * H * S * 2 + 2 * H * N * S

F32 = mybir.dt.float32
BF16 = mybir.dt.bfloat16
I32 = mybir.dt.int32
U32 = mybir.dt.uint32
U16 = mybir.dt.uint16
U8 = mybir.dt.uint8
FP8X4 = mybir.dt.float8_e4m3fn_x4
ALU = mybir.AluOpType
ACT = mybir.ActivationFunctionType

P = 128
PACK = 4
CHUNK = 128
LIST = 16
BLOCKS = 16
UPPER = P - BLOCKS
LOWER = P - 2 * BLOCKS
ROW_BYTES = 4 * S
BASE = 2 * ROW_BYTES - 128
LINE_WORDS = 4
LINE_BYTES = 16
VECTOR_SHARE = 80
WARM_PASSES = 3

PLANE = (3, 1, 2, 0)


def words_of(packed):
    return packed[0].rearrange("p n t -> p (n t)").bitcast(I32)


def tile_picked_swapgate_sigmoid_po_kernel(
    tc, x_words, x_scales, w1, w2_words, w2_scales, w3_words, w3_scales, offs, la, lb, out_0, out_1, out_2
):
    nc = tc.nc
    with ExitStack() as ctx:
        keep = ctx.enter_context(tc.tile_pool(name="keep", bufs=1))
        placed = ctx.enter_context(tc.tile_pool(name="placed", bufs=1))
        psum = ctx.enter_context(tc.psum_pool(name="psum", bufs=1))

        def sb(name, shape, dtype, reuses=None):
            return keep.tile(shape, dtype, name=name, tag=reuses or name, align_bytes=64)

        def at(name, shape, dtype, offset):
            return placed.tile(shape, dtype, name=name, offset=offset, align_bytes=64)

        def bank(number, shape):
            return psum.tile(shape, F32, name="bank%d" % number)

        offs_t = keep.tile([P, S // LIST], U16, name="offs_t")
        la_t = keep.tile([P, V // LIST], U16, name="la_t")
        lb_t = keep.tile([P, V // LIST], U16, name="lb_t")
        xw = sb("xw", [P, T], U32)
        xs = sb("xs", [P, T], U8)
        ws_raw = sb("ws_raw", [P, H], U8)
        w1_raw = [sb("w1_raw%d" % u, [P, 2, H], F32) for u in range(2)]
        gs = sb("gs", [P, S], U8)
        w2_s = sb("w2_s", [P, H], U8)
        w3_s = sb("w3_s", [P, N], U8)

        warm = sb("warm", [P, 2], F32)
        nc.gpsimd.memset(xs[0:LOWER, :].bitcast(I32), 0)
        nc.gpsimd.memset(xs[LOWER:UPPER, :].bitcast(I32), 0)
        nc.vector.memset(warm[:, 0:1], 0.0)
        nc.vector.memset(ws_raw[0:LOWER, :].bitcast(I32), 0)
        nc.vector.memset(gs[:].bitcast(I32), 0)
        nc.vector.memset(w2_s[:].bitcast(I32), 0)
        nc.vector.memset(w3_s[:].bitcast(I32), 0)
        nc.scalar.activation(warm[:, 1:2], warm[:, 0:1], ACT.Sigmoid)

        def place_scales(dst, src, first):
            for g in range(4):
                nc.sync.dma_start(dst[32 * g : 32 * g + 4, :].bitcast(I32), src[first + 4 * g : first + 4 * g + 4, :].bitcast(I32))

        w1_rows = w1.rearrange("(p j) c -> p j c", j=PACK)
        nc.sync.dma_start(offs_t[:], offs)
        nc.scalar.dma_start(xs[UPPER:P, :].bitcast(I32), x_scales[0].bitcast(I32))
        nc.sync.dma_start(xw[:].bitcast(I32), words_of(x_words))
        nc.sync.dma_start(ws_raw[LOWER:UPPER, :].bitcast(I32), w2_scales[0].bitcast(I32))
        nc.sync.dma_start(ws_raw[UPPER:P, :].bitcast(I32), w3_scales[0].bitcast(I32))
        for u in range(2):
            nc.sync.dma_start(w1_raw[u][:], w1_rows[:, 2 * u : 2 * u + 2, :])
        nc.sync.dma_start(la_t[:], la)
        nc.sync.dma_start(lb_t[:], lb)

        gs_raw = sb("gs_raw", [P, S], U8)
        nc.vector.tensor_copy(gs_raw[:], xs[:].indirect(offs_t[:]))
        place_scales(gs, gs_raw, UPPER)
        w2_raw = sb("w2_raw", [P, H], I32, reuses="xs")
        nc.sync.dma_start(w2_raw[:], words_of(w2_words))

        gw = sb("gw", [P, S], U32)
        nc.vector.tensor_copy(gw[:], xw[:].indirect(offs_t[:]))

        def deal(dst, src, run):
            nc.vector.tensor_copy(
                dst[:].rearrange("p (t b i) -> p b t i", t=PACK, i=run), src[:].rearrange("p (b i t) -> p b t i", t=PACK, i=run)
            )

        ws_dealt = sb("ws_dealt", [P, H], U8)
        deal(ws_dealt, ws_raw, LINE_BYTES)
        place_scales(w2_s, ws_dealt, LOWER)
        w3_raw = sb("w3_raw", [P, N], I32, reuses="ws_raw")
        nc.sync.dma_start(w3_raw[:], words_of(w3_words))
        place_scales(w3_s, ws_dealt, UPPER)

        w1_b = sb("w1_b", [P, PACK, P, PACK], BF16)
        w1_r = [w1_raw[u][:].rearrange("p j (m t) -> p t m j", t=PACK) for u in range(2)]
        w1_c = sb("w1_c", [P, H], U32)
        w1_s = sb("w1_s", [P, H], U8)

        def quant(codes, scales, src):
            nc.vector.quantize_mx(out=codes.bitcast(FP8X4), scales=scales, in_=src.rearrange("p s t -> p (s t)"))

        def plane_cols(t):
            return slice(P * t, P * t + P)

        for copy, ms in ((nc.vector.tensor_copy, slice(0, VECTOR_SHARE)), (nc.scalar.copy, slice(VECTOR_SHARE, P))):
            copy(w1_b[:, :, ms, 0:2].rearrange("p t m j -> p m t j"), w1_r[0][:, :, ms].rearrange("p t m j -> p m t j"))
        for copy, ms in ((nc.vector.tensor_copy, slice(0, P // 2)), (nc.scalar.copy, slice(P // 2, P))):
            copy(w1_b[:, PLANE[0], ms, 2:PACK], w1_r[1][:, PLANE[0], ms])
        planes = list(PLANE)
        nc.vector.tensor_copy(w1_b[:, planes[1], :, 2:PACK], w1_r[1][:, planes[1]])
        for t in planes[2:]:
            nc.scalar.copy(w1_b[:, t, :, 2:PACK], w1_r[1][:, t])
        for t in planes:
            quant(w1_c[:, plane_cols(t)], w1_s[:, plane_cols(t)], w1_b[:, t])

        def mm(dst, weights, weight_scales, moving, moving_scales):
            nc.tensor.matmul_mx(
                out=dst,
                lhsT=weights.bitcast(FP8X4),
                lhsT_scale=weight_scales,
                rhs=moving.bitcast(FP8X4),
                rhs_scale=moving_scales,
                start=True,
                stop=True,
            )

        y, pre, y_banks, gate_banks = {}, {}, {}, {}
        a, b, q, e, d, minus_d, z = {}, {}, {}, {}, {}, {}, {}
        halves = (slice(0, S // 2), slice(S // 2, S))
        chunks = [slice(c, c + CHUNK) for c in range(0, S, CHUNK)]
        whole = slice(0, S)

        def multiply_y(i, cols, number):
            acc = bank(number, [P, cols.stop - cols.start])
            mm(acc[:], w1_c[:, plane_cols(PLANE[i])], w1_s[:, plane_cols(PLANE[i])], gw[:, cols], gs[:, cols])
            return acc

        def multiply_gate(i, cols, number):
            acc = bank(number, [P, cols.stop - cols.start])
            mm(acc[:], w2_c[PLANE[i]], w2_s[:, plane_cols(PLANE[i])], gw[:, cols], gs[:, cols])
            return acc

        def empty(dst, acc):
            for cols in halves:
                nc.scalar.copy(dst[:, cols], acc[:, cols])

        def short(name, i, reuses=None):
            return sb("%s%d" % (name, i), [P, V], F32, reuses)

        def get_ab(i, tiles):
            a[i], b[i] = tiles
            nc.scalar.activation(a[i][:], y[i][:].indirect(la_t[:]), ACT.Copy)
            nc.scalar.activation(b[i][:], y[i][:].indirect(lb_t[:]), ACT.Copy)

        def get_q(i, tile=None):
            q[i] = short("q", i) if tile is None else tile
            nc.scalar.activation(q[i][:], pre[i][:].indirect(la_t[:]), ACT.Sigmoid)

        def get_e(i, reuses=None):
            e[i] = short("e", i, reuses)
            nc.vector.tensor_tensor(e[i][:], b[i][:], a[i][:], ALU.subtract)

        def get_d(i):
            d[i] = short("d", i)
            nc.vector.tensor_tensor(d[i][:], q[i][:], e[i][:], ALU.mult)

        def negate_d(i, reuses=None):
            minus_d[i] = short("minus_d", i, reuses)
            nc.scalar.activation(minus_d[i][:], d[i][:], ACT.Copy, scale=-1.0)

        def put_na(i):
            nc.vector.tensor_tensor(z[i][:].indirect(la_t[:]), a[i][:], d[i][:], ALU.add)

        def put_nb(i):
            nc.vector.tensor_tensor(z[i][:].indirect(lb_t[:]), b[i][:], minus_d[i][:], ALU.add)

        def weave(i, copies):
            n = S // len(copies)
            pair = z[i][:].rearrange("p (r s) -> p s r", r=2)
            for c, copy in enumerate(copies):
                copy(z_b[:, n * c : n * c + n, PLANE[i] : PLANE[i] + 2], pair[:, n * c : n * c + n, :])

        na, nb = {}, {}

        def two(engine, out, left, right, op):
            engine.tensor_tensor(out[:], left[:], right[:], op)
            return out

        def put(i, offsets, values):
            nc.vector.tensor_copy(z[i][:].indirect(offsets[:]), values[:])

        def gather(i, offsets, out):
            nc.vector.tensor_copy(out[:], y[i][:].indirect(offsets[:]))
            return out

        y[0] = sb("y0", [P, S], F32)
        for number, (copy, cols) in enumerate(zip((nc.scalar.copy, nc.scalar.copy, nc.vector.tensor_copy), (halves[0], chunks[2], chunks[3]))):
            copy(y[0][:, cols], multiply_y(0, cols, number)[:])
        w2_planes = w2_raw[:].rearrange("p (b i t) -> p b t i", t=PACK, i=LINE_WORDS)
        w2_first = at("w2_first", [P, P], I32, 5 * ROW_BYTES)
        nc.vector.tensor_copy(w2_first[:].rearrange("p (b i) -> p b i", i=LINE_WORDS), w2_planes[:, :, PACK - 1, :])
        w2_rest = sb("w2_rest", [P, PACK - 1, P], I32)
        nc.vector.tensor_copy(w2_rest[:].rearrange("p t (b i) -> p b t i", i=LINE_WORDS), w2_planes[:, :, 0 : PACK - 1, :])
        w2_c = [w2_rest[:, t, :] for t in range(PACK - 1)] + [w2_first[:]]
        y_banks[1] = multiply_y(1, whole, 3)
        y_banks[2] = [multiply_y(2, cols, number) for cols, number in zip(halves, (4, 0))]
        def pair(name, reuses=None):
            return sb(name, [P, 2, V], F32, reuses)

        def fetch(out, window, offsets, func=ACT.Copy):
            nc.scalar.activation(out, window[:].indirect(offsets[:]), func)

        y[1] = sb("y1", [P, S], F32)
        empty(y[1], y_banks[1])
        a[0], a[1], b[0] = short("a", 0), short("a", 1), short("b", 0)
        gather(0, la_t, a[0])
        fetch(b[0][:], y[0], lb_t)
        gather(1, la_t, a[1])
        get_e(0)
        pre[0] = at("pre0", [P, S], F32, 0)
        for cols, number in zip(halves, (6, 7)):
            nc.scalar.activation(pre[0][:, cols], multiply_gate(0, cols, number)[:], ACT.Sigmoid)
        gate_banks[1] = [multiply_gate(1, cols, number) for cols, number in zip(halves, (1, 7))]
        gate_banks[2] = multiply_gate(2, whole, 2)
        gate_banks[3] = [multiply_gate(3, cols, number) for cols, number in zip(halves, (5, 3))]
        b[1] = at("b1", [P, V], F32, 5 * ROW_BYTES + 256)
        fetch(b[1][:], y[1], lb_t)
        pre[1] = at("pre1", [P, S], F32, 2 * ROW_BYTES)
        for cols, acc in zip(halves, gate_banks[1]):
            nc.scalar.copy(pre[1][:, cols], acc[:])
        get_q(1)

        y[2] = at("y2", [P, S], F32, 4 * ROW_BYTES + 256)
        nc.vector.tensor_copy(y[2][:, halves[0]], y_banks[2][0][:])
        d[0] = short("d", 0)
        nc.vector.tensor_tensor(d[0][:], pre[0][:].indirect(la_t[:]), e[0][:], ALU.mult)
        get_e(1)
        na[0] = two(nc.vector, short("na", 0), a[0], d[0], ALU.add)
        y_banks[3] = [multiply_y(3, cols, number) for cols, number in zip(halves, (6, 7))]
        nb[0] = two(nc.vector, short("nb", 0), b[0], d[0], ALU.subtract)
        z[0] = sb("z0", [P, S], F32)
        put(0, la_t, na[0])

        y[3] = sb("y3", [P, S], F32, reuses="b0")
        nc.vector.tensor_copy(y[3][:, halves[0]], y_banks[3][0][:])
        put(0, lb_t, nb[0])
        d[1] = two(nc.gpsimd, short("d", 1, reuses="d0"), q[1], e[1], ALU.mult)
        na[1] = two(nc.gpsimd, short("na", 1), a[1], d[1], ALU.add)
        z[1] = sb("z1", [P, S], F32)
        put(1, la_t, na[1])
        nb[1] = two(nc.gpsimd, short("nb", 1, reuses="a1"), b[1], d[1], ALU.subtract)
        pre[3] = at("pre3", [P, S], F32, 5 * ROW_BYTES + 256)
        nc.vector.tensor_copy(pre[3][:, halves[0]], gate_banks[3][0][:])
        put(1, lb_t, nb[1])

        a_late, b_late = pair("a_late"), pair("b_late")
        for i in (2, 3):
            a[i], b[i] = a_late[:, i - 2, :], b_late[:, i - 2, :]
            nc.scalar.copy(y[i][:, halves[1]], y_banks[i][1][:])
            fetch(a[i], y[i], la_t)
            fetch(b[i], y[i], lb_t)
        pre[2] = at("pre2", [P, S], F32, ROW_BYTES + 64)
        empty(pre[2], gate_banks[2])
        nc.scalar.copy(pre[3][:, halves[1]], gate_banks[3][1][:])
        for i in (2, 3):
            get_q(i)
        e_late = two(nc.gpsimd, pair("e_late", reuses="d0"), b_late, a_late, ALU.subtract)
        d[2] = two(nc.gpsimd, short("d", 2), q[2], e_late[:, 0, :], ALU.mult)
        d[3] = two(nc.vector, short("d", 3, reuses="q2"), q[3], e_late[:, 1, :], ALU.mult)
        for i in (2, 3):
            negate_d(i)
        for i in (2, 3):
            z[i] = sb("z%d" % i, [P, 2 * S], F32)
            put_na(i)
            nc.scalar.copy(z[i][:, S : 2 * S], z[i - 2][:])
        put_nb(2)

        def deal_w3(copy, dtype, name, planes, reuses):
            dealt = sb(name, [P, len(planes), P], dtype, reuses)
            source = w3_raw[:].bitcast(dtype).rearrange("p (b i t) -> p b t i", t=PACK, i=LINE_WORDS)
            copy(dealt[:].rearrange("p t (b i) -> p b t i", i=LINE_WORDS), source[:, :, planes.start : planes.stop, :])
            return [dealt[:, j, :] for j in range(len(planes))]

        w3_c = deal_w3(nc.scalar.copy, U32, "w3_rest", range(1, PACK), "q3")
        w3_c = deal_w3(nc.scalar.copy, U32, "w3_first", range(1), "z1") + w3_c
        z_b = sb("z_b", [P, S, PACK], BF16, reuses="ws_raw")
        weave(2, [nc.scalar.copy])
        idle = bank(0, [P, S])
        for warm_pass in range(WARM_PASSES):
            mm(idle[:], w3_c[0], w3_s[:, plane_cols(0)], gw[:], gs[:])
        put_nb(3)
        weave(3, [nc.vector.tensor_copy] * 2 + [nc.scalar.copy] * 2)

        z_s = sb("z_s", [P, S], U8)
        o_b = sb("o_b", [P, S, PACK], BF16)
        o_c = sb("o_c", [P, S], U32)
        o_s = sb("o_s", [P, S], U8)
        out_rows = out_0.rearrange("(p t) s -> p t s", t=PACK)
        out_words = words_of(out_1)

        o = [sb("o%d" % c, [P, PACK, CHUNK], F32)[:] for c in range(len(chunks))]
        z_c = sb("z_c", [P, S], U32)
        for cols in chunks:
            quant(z_c[:, cols], z_s[:, cols], z_b[:, cols, :])
        def multiply_out(c, planes):
            acc = bank((1 + 2 * c + planes[0] // 2) % 8, [P, len(planes), CHUNK])
            for j, t in enumerate(planes):
                mm(acc[:, j, :], w3_c[t], w3_s[:, plane_cols(t)], z_c[:, chunks[c]], z_s[:, chunks[c]])
            return acc

        for c in range(3):
            for first in (0, 2):
                copy = nc.vector.tensor_copy if c < 2 and first else nc.scalar.copy
                copy(o[c][:, first : first + 2, :], multiply_out(c, (first, first + 1))[:])
            nc.sync.dma_start(out_rows[:, :, chunks[c]], o[c])
        last_bank = multiply_out(3, range(PACK))
        nc.scalar.copy(o[3], last_bank[:])
        nc.sync.dma_start(out_rows[:, :, chunks[3]], o[3])

        for c in range(3):
            nc.vector.tensor_copy(o_b[:, chunks[c], :], o[c].rearrange("p t s -> p s t"))
        nc.scalar.copy(o_b[:, chunks[3], :], last_bank[:].rearrange("p t s -> p s t"))
        for cols in (halves[0], chunks[2], chunks[3]):
            quant(o_c[:, cols], o_s[:, cols], o_b[:, cols, :])
        nc.sync.dma_start(out_words, o_c[:].bitcast(I32))
        for g in range(4):
            queue = nc.scalar if g % 2 else nc.sync
            queue.dma_start(out_2[0, 4 * g : 4 * g + 4, :].bitcast(I32), o_s[32 * g : 32 * g + 4, :].bitcast(I32))
